import numpy as np
import ml_dtypes


def mxq(x, axis, fmt="e4m3"):
    dtype, down = {"e4m3": (ml_dtypes.float8_e4m3fn, 7), "e5m2": (ml_dtypes.float8_e5m2, 14)}[fmt]
    v = np.moveaxis(np.asarray(x, np.float32).astype(ml_dtypes.bfloat16).astype(np.float64), axis, -1)
    blocks = v.reshape(v.shape[:-1] + (-1, 32))
    amax = np.abs(blocks).max(-1, keepdims=True)
    byte = np.maximum(np.where(amax > 0, np.frexp(amax)[1] - 1 + 127, 0) - down, 1)
    scale = np.exp2(byte - 127.0)
    codes = (blocks / scale).astype(np.float32).astype(dtype).astype(np.float64)
    return np.moveaxis((codes * scale).reshape(v.shape), -1, axis)


WIDE = False


def mx_kscale(k):
    if not WIDE:
        return np.ones(k)
    levels = np.array([10, -10, 5, -5, 0])
    if k % 512:
        return np.exp2(np.random.permutation(np.resize(levels, k // 32))).repeat(32)
    a = np.empty((k // 512, 16))
    for p in range(k // 512):
        a[p, :8] = np.random.permutation(np.resize(levels, 8))
        for g in range(8):
            far = levels[np.abs(levels - a[p, g]) >= 10]
            a[p, g + 8] = far[np.random.randint(len(far))]
    return np.exp2(a.ravel()).repeat(32)


BF16 = ml_dtypes.bfloat16


def bf(x):
    return np.asarray(x, np.float32).astype(BF16)


def f64(x):
    return np.asarray(x).astype(np.float64)


T, K, N, S = 2048, 1024, 512, 512

REWARD_STD = 0.7
REWARD_BIAS_STD = 0.3
CONT_BIAS_STD = 0.5
BOOT_STD = 0.7


def sigmoid(z):
    return 0.5 * (1.0 + np.tanh(0.5 * z))


def symexp(z):
    return np.tanh(0.5 * z) * (np.exp(np.abs(z)) + 1.0)


def symlog(z):
    return np.sign(z) * np.log(1.0 + np.abs(z))


def draw0():
    s = mx_kscale(K)
    u = mx_kscale(T)
    return {"x": bf(np.random.standard_normal((T, K)) * s),
            "w_reward": bf(REWARD_STD * np.random.standard_normal((K, N)) / np.sqrt(K) / s[:, None]),
            "w_cont": bf(np.random.standard_normal((K, N)) / np.sqrt(K) / s[:, None]),
            "b_reward": bf(REWARD_BIAS_STD * np.random.standard_normal(N)),
            "b_cont": bf(CONT_BIAS_STD * np.random.standard_normal(N)),
            "step_weight": bf(np.random.uniform(0.5, 1.5, T) * u),
            "filters": bf(np.random.standard_normal((S, T)) / np.sqrt(T) / u),
            "boot": bf(BOOT_STD * np.random.standard_normal((S, N)))}


def core(x, w_reward, w_cont, b_reward, b_cont, step_weight, filters, boot):
    xq = mxq(f64(x), 1, "e4m3")
    zr = (xq @ mxq(f64(w_reward), 0, "e4m3")) + f64(b_reward)
    zc = (xq @ mxq(f64(w_cont), 0, "e4m3")) + f64(b_cont)
    c = f64(step_weight)[:, None] * sigmoid(zc)
    y = c * symexp(zr)
    pq = mxq(f64(filters), 1, "e4m3")
    mass = pq @ mxq(c, 0, "e4m3")
    gain = pq @ mxq(y, 0, "e4m3")
    ret = symlog(gain + mass * f64(boot))
    return ret, mass


def e4m3fn_bytes(y):
    return np.clip(np.asarray(y, np.float64), -448.0, 448.0).astype(np.float32).astype(ml_dtypes.float8_e4m3fn).view(np.uint8)


def e4m3fn_values(b):
    return np.asarray(b, np.uint8).view(ml_dtypes.float8_e4m3fn).astype(np.float64)


def setup_inputs():
    d = draw0()
    x0 = np.asarray(d['x']).astype(np.float64)
    s = (np.max(np.abs(x0), axis=(0,), keepdims=True) / 448.0).astype(np.float32)
    out = {}
    for k, v in d.items():
        if k == 'x':
            out['x_bytes'] = e4m3fn_bytes(x0 / s.astype(np.float64))
            out['x_scale'] = s
        else:
            out[k] = v
    return out


def reference(x_bytes, x_scale, w_reward, w_cont, b_reward, b_cont, step_weight, filters, boot):
    return core(e4m3fn_values(x_bytes) * x_scale.astype(np.float64), w_reward, w_cont, b_reward, b_cont, step_weight, filters, boot)

@@ -1,0 +1,367 @@
+from contextlib import ExitStack
+
+import concourse.mybir as mybir
+from concourse.masks import make_identity
+
+F32 = mybir.dt.float32
+BF16 = mybir.dt.bfloat16
+U32 = mybir.dt.uint32
+U8 = mybir.dt.uint8
+FP8 = mybir.dt.float8_e4m3fn
+FP8X4 = mybir.dt.float8_e4m3fn_x4
+ACT = mybir.ActivationFunctionType
+ALU = mybir.AluOpType
+
+P = 128
+T, K, N, S = 2048, 1024, 512, 512
+G = T // 512
+KP = K // 512
+J = N // P
+UNITS = J * G
+
+FLOPS = 2 * T * K * 2 * N + 2 * S * T * 2 * N
+
+
+def tile_reward_continuation_returns_f4_kernel(
+    tc, x_bytes, x_scale, w_reward, w_cont, b_reward, b_cont, step_weight, filters, boot, out_0, out_1
+):
+    nc = tc.nc
+    with ExitStack() as ctx:
+        keep = ctx.enter_context(tc.tile_pool(name="keep", bufs=1))
+        work = ctx.enter_context(tc.tile_pool(name="work", bufs=2))
+        psum = ctx.enter_context(tc.psum_pool(name="psum", bufs=1))
+
+        ident = keep.tile([P, P], F32)
+        ident_bf = keep.tile([P, P], BF16)
+        warm = keep.tile([P, 1], F32)
+        b_rows = keep.tile([P, P], BF16)
+        bias = keep.tile([P, 3 * J], F32)
+        scale = keep.tile([P, K], F32)
+        sw = keep.tile([P, T], BF16)
+        sw_cols = keep.tile([P, T], BF16)
+        boot_sb = keep.tile([P, S // P, N], BF16)
+        xb = [keep.tile([P, 4, K], U8, name="xb%d" % g) for g in range(G)]
+        w_raw = [keep.tile([P, 4, N], BF16, name="w_raw%d" % i) for i in range(2 * KP)]
+        f_raw = [keep.tile([P, T], BF16, name="f_raw%d" % i) for i in range(S // P)]
+        f_in = keep.tile([P, G, S, 4], BF16, align_bytes=64)
+        x_codes = keep.tile([P, G * KP, 512], U32, align_bytes=64)
+        x_scales = keep.tile([P, G * KP, 512], U8, align_bytes=64)
+        w_codes = keep.tile([P, 2 * KP, N], U32, align_bytes=64)
+        w_scales = keep.tile([P, 2 * KP, N], U8, align_bytes=64)
+        f_codes = keep.tile([P, G, S], U32, align_bytes=64)
+        f_scales = keep.tile([P, G, S], U8, align_bytes=64)
+        log_sb = keep.tile([P, S // P, N], F32)
+        sign_sb = keep.tile([P, S // P, N], F32)
+
+        ctx.enter_context(tc.manual_schedule())
+
+        xv = x_bytes.rearrange("(g p s) k -> g p s k", p=P, s=4)
+        wv = [w.rearrange("(q p j) n -> q p j n", p=P, j=4) for w in (w_cont, w_reward)]
+        nc.vector.memset(b_rows[:], 0.0)
+        nc.vector.memset(warm[:], 0.0)
+        nc.scalar.dma_start(out=scale[:], in_=x_scale.rearrange("o k -> (o k)").partition_broadcast(P))
+        nc.scalar.activation(out=warm[:], in_=warm[:], func=ACT.Exp)
+        nc.sync.dma_start(out=xb[0][:, 0:2, :], in_=xv[0][:, 0:2, :])
+        nc.sync.dma_start(out=xb[0][:, 2:4, :], in_=xv[0][:, 2:4, :])
+        nc.sync.dma_start(out=w_raw[0][:], in_=wv[0][0])
+        nc.sync.dma_start(out=w_raw[1][:], in_=wv[1][0])
+        nc.sync.dma_start(out=xb[1][:], in_=xv[1])
+        nc.sync.dma_start(out=b_rows[0:4, :], in_=b_reward.rearrange("(c p) -> c p", p=P))
+        nc.sync.dma_start(out=b_rows[4:8, :], in_=b_cont.rearrange("(c p) -> c p", p=P))
+        nc.sync.dma_start(out=w_raw[2][:], in_=wv[0][1])
+        nc.sync.dma_start(out=w_raw[3][:], in_=wv[1][1])
+        nc.sync.dma_start(out=xb[2][:], in_=xv[2])
+        nc.sync.dma_start(out=f_raw[0][:], in_=filters[0:P, :])
+        nc.sync.dma_start(out=f_raw[1][:], in_=filters[P : 2 * P, :])
+        nc.sync.dma_start(out=xb[3][:], in_=xv[3])
+        nc.sync.dma_start(out=f_raw[2][:], in_=filters[2 * P : 3 * P, :])
+        nc.sync.dma_start(out=f_raw[3][:], in_=filters[3 * P : 4 * P, :])
+        nc.sync.dma_start(out=sw[:], in_=step_weight.partition_broadcast(P))
+        nc.sync.dma_start(out=boot_sb[:], in_=boot.rearrange("(i p) n -> p i n", p=P))
+
+        make_identity(nc, ident[:])
+        make_identity(nc, ident_bf[:])
+
+        def bank(shape, dtype=F32):
+            return psum.tile(shape, dtype, tag="bank", bufs=6, name="bank")
+
+        xp = {}
+        xi = {}
+
+        def x_product(g, s):
+            t = work.tile([P, K], BF16, tag="xp", bufs=4, name="xp")
+            nc.vector.tensor_tensor(out=t[:], in0=xb[g][:, s, :].bitcast(FP8), in1=scale[:], op=ALU.mult)
+            xp[g, s] = t
+
+        def x_turn(g, h):
+            for q in range(KP):
+                if h == 0:
+                    xi[g, q] = work.tile([P, 512, 4], BF16, tag="xi", bufs=4, align_bytes=64, name="xi")
+                b = bank([P, 4, P])
+                for e in range(2):
+                    words = xp[g, 2 * h + e][:].bitcast(F32)
+                    for u in range(2):
+                        nc.tensor.transpose(b[:, 2 * e + u, :], words[:, 256 * q + u : 256 * (q + 1) : 2], ident[:])
+                out_words = xi[g, q][:].rearrange("p c t -> p (c t)").bitcast(F32)[:, 512 * h : 512 * (h + 1)]
+                nc.scalar.copy(
+                    out=out_words.rearrange("p (c w) -> p c w", w=4), in_=b[:].rearrange("p w c -> p c w")
+                )
+
+        def x_quant(g):
+            for q in range(KP):
+                nc.vector.quantize_mx(
+                    out=x_codes[:, KP * g + q, :].bitcast(FP8X4),
+                    scales=x_scales[:, KP * g + q, :],
+                    in_=xi[g, q][:].rearrange("p c t -> p (c t)"),
+                )
+
+        wi = {}
+
+        def w_interleave(i):
+            t = work.tile([P, N, 4], BF16, tag="wi", bufs=2, align_bytes=64, name="wi")
+            nc.scalar.copy(out=t[:], in_=w_raw[i][:].rearrange("p j n -> p n j"))
+            wi[i] = t
+
+        def w_quant(i):
+            nc.vector.quantize_mx(
+                out=w_codes[:, i, :].bitcast(FP8X4),
+                scales=w_scales[:, i, :],
+                in_=wi[i][:].rearrange("p n j -> p (n j)"),
+            )
+
+        f_words = f_in[:].rearrange("p g s t -> p (g s t)").bitcast(F32).rearrange("p (g s u) -> p g s u", g=G, u=2)
+
+        def f_turn(i, h):
+            words = f_raw[i][:].bitcast(F32)
+            b = bank([P, 4, P])
+            for g in range(2):
+                for u in range(2):
+                    first = 256 * (2 * h + g)
+                    nc.tensor.transpose(b[:, 2 * g + u, :], words[:, first + u : first + 256 : 2], ident[:])
+            nc.scalar.copy(
+                out=f_words[:, 2 * h : 2 * h + 2, P * i : P * (i + 1), :],
+                in_=b[:].rearrange("p (g u) s -> p g s u", u=2),
+            )
+
+        def f_quant(g):
+            nc.vector.quantize_mx(
+                out=f_codes[:, g, :].bitcast(FP8X4),
+                scales=f_scales[:, g, :],
+                in_=f_in[:, g, :, :].rearrange("p s t -> p (s t)"),
+            )
+
+        zc, zr, th, e1, e2, cy, tb, cyi = {}, {}, {}, {}, {}, {}, {}, {}
+        cy_codes, cy_scales = {}, {}
+
+        def heads(k):
+            j, g = k // G, k % G
+            cols = slice(P * j, P * (j + 1))
+            for head, store in ((0, zc), (1, zr)):
+                b = bank([P, 512])
+                for q in range(KP):
+                    nc.tensor.matmul_mx(
+                        out=b[:],
+                        lhsT=w_codes[:, 2 * q + head, cols].bitcast(FP8X4),
+                        lhsT_scale=w_scales[:, 2 * q + head, cols],
+                        rhs=x_codes[:, KP * g + q, :].bitcast(FP8X4),
+                        rhs_scale=x_scales[:, KP * g + q, :],
+                        start=(q == 0),
+                        stop=(q == KP - 1),
+                    )
+                store[k] = b
+
+        def act_tanh(k):
+            j = k // G
+            t = work.tile([P, 512], F32, tag="th", bufs=2, name="th")
+            nc.scalar.activation(out=t[:], in_=zc[k][:], func=ACT.Tanh, bias=bias[:, J + j : J + j + 1], scale=0.5)
+            th[k] = t
+
+        def act_exp(k):
+            j = k // G
+            t = work.tile([P, 512], F32, tag="e2", bufs=3, name="e2")
+            nc.scalar.activation(out=t[:], in_=zr[k][:], func=ACT.Exp, bias=bias[:, 2 * J + j : 2 * J + j + 1], scale=-1.0)
+            e2[k] = t
+            t = work.tile([P, 512], F32, tag="e1", bufs=3, name="e1")
+            nc.scalar.activation(out=t[:], in_=zr[k][:], func=ACT.Exp, bias=bias[:, j : j + 1], scale=1.0)
+            e1[k] = t
+
+        def epilogue(k):
+            g = k % G
+            e2m = work.tile([P, 512], F32, tag="e2m", bufs=2, name="e2m")
+            nc.vector.tensor_scalar(out=e2m[:], in0=e2[k][:], scalar1=1.0, scalar2=None, op0=ALU.max)
+            c2 = work.tile([P, 512], F32, tag="c2", bufs=2, name="c2")
+            nc.vector.scalar_tensor_tensor(
+                out=c2[:], in0=th[k][:], scalar=1.0, in1=sw_cols[:, 512 * g : 512 * (g + 1)], op0=ALU.add, op1=ALU.mult
+            )
+            dd = work.tile([P, 512], F32, tag="dd", bufs=2, name="dd")
+            nc.vector.scalar_tensor_tensor(
+                out=dd[:], in0=e1[k][:], scalar=1.0, in1=e2m[:], op0=ALU.max, op1=ALU.subtract
+            )
+            t = work.tile([P, 2, 512], BF16, tag="cy", bufs=3, name="cy")
+            nc.vector.tensor_scalar(out=t[:, 0, :], in0=c2[:], scalar1=0.5, scalar2=None, op0=ALU.mult)
+            nc.vector.scalar_tensor_tensor(
+                out=t[:, 1, :], in0=c2[:], scalar=0.5, in1=dd[:], op0=ALU.mult, op1=ALU.mult
+            )
+            cy[k] = t
+
+        def turn(k):
+            words = cy[k][:].rearrange("p i c -> p (i c)").bitcast(F32)
+            b = bank([P, 4, P])
+            for w in range(4):
+                nc.tensor.transpose(b[:, w, :], words[:, P * w : P * (w + 1)], ident[:])
+            tb[k] = b
+
+        def turn_out(k):
+            t = work.tile([P, 2, P, 4], BF16, tag="cyi", bufs=3, align_bytes=64, name="cyi")
+            out_words = t[:].rearrange("p i n t -> p (i n t)").bitcast(F32)
+            nc.scalar.copy(
+                out=out_words.rearrange("p (i n h) -> p i n h", i=2, h=2),
+                in_=tb[k][:].rearrange("p (i h) n -> p i n h", h=2),
+            )
+            cyi[k] = t
+
+        def turn_quant(k):
+            j, g = k // G, k % G
+            if g == 0:
+                cy_codes[j] = work.tile([P, G, 2 * P], U32, tag="cy_codes", bufs=2, align_bytes=64, name="cy_codes")
+                cy_scales[j] = work.tile([P, G, 2 * P], U8, tag="cy_scales", bufs=2, align_bytes=64, name="cy_scales")
+            nc.vector.quantize_mx(
+                out=cy_codes[j][:, g, :].bitcast(FP8X4),
+                scales=cy_scales[j][:, g, :],
+                in_=cyi[k][:].rearrange("p i n t -> p (i n t)"),
+            )
+
+        acc = {}
+
+        def filter_pass(j, i, g, out):
+            nc.tensor.matmul_mx(
+                out=out,
+                lhsT=f_codes[:, g, P * i : P * (i + 1)].bitcast(FP8X4),
+                lhsT_scale=f_scales[:, g, P * i : P * (i + 1)],
+                rhs=cy_codes[j][:, g, :].bitcast(FP8X4),
+                rhs_scale=cy_scales[j][:, g, :],
+                start=(g == 0),
+                stop=(g == G - 1),
+            )
+
+        def filter_sums(j, i):
+            if i % 2 == 0:
+                acc[j, i // 2] = psum.tile([P, 2, 2 * P], F32, tag="acc", bufs=2, name="acc")
+            for g in range(G):
+                filter_pass(j, i, g, acc[j, i // 2][:, i % 2, :])
+
+        mass_out = out_1.rearrange("(i p) n -> p i n", p=P)
+        ret_out = out_0.rearrange("(i p) n -> p i n", p=P)
+
+        def finish(j, rows, a):
+            n = rows.stop - rows.start
+            cols = slice(P * j, P * (j + 1))
+            ms = work.tile([P, n, P], F32, tag="ms%d" % n, bufs=2, name="ms")
+            nc.scalar.copy(out=ms[:], in_=a[:, :, 0:P])
+            nc.sync.dma_start(out=mass_out[:, rows, cols], in_=ms[:])
+            t1 = work.tile([P, n, P], F32, tag="t1%d" % n, bufs=2, name="t1")
+            nc.vector.tensor_tensor(out=t1[:], in0=a[:, :, 0:P], in1=boot_sb[:, rows, cols], op=ALU.mult)
+            t2 = work.tile([P, n, P], F32, tag="t2%d" % n, bufs=2, name="t2")
+            nc.vector.tensor_tensor(out=t2[:], in0=a[:, :, P : 2 * P], in1=t1[:], op=ALU.add)
+            nc.scalar.activation(out=log_sb[:, rows, cols], in_=t2[:], func=ACT.Abs)
+            nc.scalar.activation(out=sign_sb[:, rows, cols], in_=t2[:], func=ACT.Sign)
+
+        def symlog(rows, cols):
+            nc.scalar.activation(out=log_sb[:, rows, cols], in_=log_sb[:, rows, cols], func=ACT.Ln, bias=1.0, scale=1.0)
+
+        def symlog_store(rows, cols):
+            nc.vector.tensor_tensor(
+                out=log_sb[:, rows, cols], in0=log_sb[:, rows, cols], in1=sign_sb[:, rows, cols], op=ALU.mult
+            )
+            nc.sync.dma_start(out=ret_out[:, rows, cols], in_=log_sb[:, rows, cols])
+
+        for g in range(G):
+            x_product(g, 0)
+            x_product(g, 1)
+            if g == 0:
+                w_interleave(0)
+            x_turn(g, 0)
+            if g == 0:
+                w_interleave(1)
+            if g == 1:
+                w_interleave(2)
+            x_product(g, 2)
+            x_product(g, 3)
+            x_turn(g, 1)
+            if g == 1:
+                w_quant(0)
+                w_quant(1)
+                w_interleave(3)
+            if g == 2:
+                w_quant(2)
+                b_t = bank([P, P], BF16)
+                nc.tensor.transpose(b_t[:], b_rows[:], ident_bf[:])
+                nc.vector.tensor_scalar(out=bias[:, 0:J], in0=b_t[:, 0:J], scalar1=1.0, scalar2=None, op0=ALU.mult)
+                nc.vector.tensor_scalar(
+                    out=bias[:, J : 2 * J], in0=b_t[:, J : 2 * J], scalar1=0.5, scalar2=None, op0=ALU.mult
+                )
+                nc.vector.tensor_scalar(
+                    out=bias[:, 2 * J : 3 * J], in0=b_t[:, 0:J], scalar1=-1.0, scalar2=None, op0=ALU.mult
+                )
+                w_quant(3)
+            if g > 0:
+                x_quant(g - 1)
+            if g >= 2:
+                for i in (2 * g - 4, 2 * g - 3):
+                    f_turn(i, 0)
+                    f_turn(i, 1)
+            if g == 3:
+                nc.scalar.copy(
+                    out=sw_cols[:].bitcast(F32).rearrange("p (g h c) -> p g h c", g=G, h=2),
+                    in_=sw[:].bitcast(F32).rearrange("p (g c h) -> p g h c", g=G, h=2),
+                )
+        heads(0)
+        heads(1)
+        act_tanh(0)
+        act_exp(0)
+        x_quant(G - 1)
+        for g in range(G):
+            f_quant(g)
+
+        all_rows = slice(0, S // P)
+        tail = {}
+        for k in range(UNITS + 1):
+            if 1 <= k:
+                turn(k - 1)
+            if k + 2 < UNITS:
+                heads(k + 2)
+            if k + 1 < UNITS:
+                act_tanh(k + 1)
+            if 1 <= k:
+                turn_out(k - 1)
+            if k + 1 < UNITS:
+                act_exp(k + 1)
+            if k < UNITS:
+                epilogue(k)
+            if 1 <= k:
+                turn_quant(k - 1)
+            if k <= 12 and k >= 5:
+                j, i = (k - 5) // 4, (k - 5) % 4
+                filter_sums(j, i)
+                if i % 2 == 1:
+                    finish(j, slice(i - 1, i + 1), acc[j, i // 2][:])
+            if k == 13 or k == 14:
+                i = 2 * (k - 13)
+                filter_sums(2, i)
+                filter_sums(2, i + 1)
+                finish(2, slice(i, i + 2), acc[2, i // 2][:])
+            if k == 15:
+                for i in range(S // P):
+                    tail[i] = bank([P, 1, 2 * P])
+                    filter_pass(3, i, 0, tail[i][:, 0, :])
+                    filter_pass(3, i, 1, tail[i][:, 0, :])
+                symlog(all_rows, slice(0, 3 * P))
+            if k == 16:
+                for i in range(S // P):
+                    filter_pass(3, i, 2, tail[i][:, 0, :])
+                symlog_store(all_rows, slice(0, 3 * P))
+                for i in range(S // P):
+                    filter_pass(3, i, 3, tail[i][:, 0, :])
+                    finish(3, slice(i, i + 1), tail[i][:])
+                symlog(all_rows, slice(3 * P, 4 * P))
+                symlog_store(all_rows, slice(3 * P, 4 * P))

@@ -18,6 +18,10 @@ G = T // 512
 KP = K // 512
 J = N // P
 UNITS = J * G
+ORDER = [(j, 2 * half + i) for half in range(2) for j in range(2) for i in range(2)] + [(j, g) for j in (2, 3) for g in range(G)]
+SUMS = {7: (0, 0), 8: (0, 2), 9: (1, 0), 10: (1, 2), 13: (2, 0), 14: (2, 2)}
+FINISH = {8: (0, 0), 9: (0, 1), 10: (1, 0), 11: (1, 1), 14: (2, 0)}
+CAST_ON_SCALAR = tuple(range(6))
 
 FLOPS = 2 * T * K * 2 * N + 2 * S * T * 2 * N
 
@@ -36,13 +40,13 @@ def tile_reward_continuation_returns_f4_kernel(
         warm = keep.tile([P, 1], F32)
         b_rows = keep.tile([P, P], BF16)
         bias = keep.tile([P, 3 * J], F32)
-        scale = keep.tile([P, K], F32)
+        scale_raw = keep.tile([P, KP, 4], F32)
+        scale = keep.tile([P, KP, 4, 2], F32)
         sw = keep.tile([P, T], BF16)
-        sw_cols = keep.tile([P, T], BF16)
         boot_sb = keep.tile([P, S // P, N], BF16)
         xb = [keep.tile([P, 4, K], U8, name="xb%d" % g) for g in range(G)]
-        w_raw = [keep.tile([P, 4, N], BF16, name="w_raw%d" % i) for i in range(2 * KP)]
-        f_raw = [keep.tile([P, T], BF16, name="f_raw%d" % i) for i in range(S // P)]
+        w_raw = [work.tile([P, 4, N], BF16, tag="raw", bufs=6, name="w_raw") for i in range(2 * KP)]
+        f_raw = {}
         f_in = keep.tile([P, G, S, 4], BF16, align_bytes=64)
         x_codes = keep.tile([P, G * KP, 512], U32, align_bytes=64)
         x_scales = keep.tile([P, G * KP, 512], U8, align_bytes=64)
@@ -59,74 +63,99 @@ def tile_reward_continuation_returns_f4_kernel(
         wv = [w.rearrange("(q p j) n -> q p j n", p=P, j=4) for w in (w_cont, w_reward)]
         nc.vector.memset(b_rows[:], 0.0)
         nc.vector.memset(warm[:], 0.0)
-        nc.scalar.dma_start(out=scale[:], in_=x_scale.rearrange("o k -> (o k)").partition_broadcast(P))
+        nc.scalar.dma_start(out=scale_raw[:], in_=x_scale.rearrange("o (q p t) -> p (o q) t", p=P, t=4))
         nc.scalar.activation(out=warm[:], in_=warm[:], func=ACT.Exp)
         nc.sync.dma_start(out=xb[0][:, 0:2, :], in_=xv[0][:, 0:2, :])
         nc.sync.dma_start(out=xb[0][:, 2:4, :], in_=xv[0][:, 2:4, :])
         nc.sync.dma_start(out=w_raw[0][:], in_=wv[0][0])
-        nc.sync.dma_start(out=w_raw[1][:], in_=wv[1][0])
         nc.sync.dma_start(out=xb[1][:], in_=xv[1])
+        nc.sync.dma_start(out=w_raw[1][:], in_=wv[1][0])
         nc.sync.dma_start(out=b_rows[0:4, :], in_=b_reward.rearrange("(c p) -> c p", p=P))
         nc.sync.dma_start(out=b_rows[4:8, :], in_=b_cont.rearrange("(c p) -> c p", p=P))
         nc.sync.dma_start(out=w_raw[2][:], in_=wv[0][1])
-        nc.sync.dma_start(out=w_raw[3][:], in_=wv[1][1])
         nc.sync.dma_start(out=xb[2][:], in_=xv[2])
-        nc.sync.dma_start(out=f_raw[0][:], in_=filters[0:P, :])
-        nc.sync.dma_start(out=f_raw[1][:], in_=filters[P : 2 * P, :])
-        nc.sync.dma_start(out=xb[3][:], in_=xv[3])
-        nc.sync.dma_start(out=f_raw[2][:], in_=filters[2 * P : 3 * P, :])
-        nc.sync.dma_start(out=f_raw[3][:], in_=filters[3 * P : 4 * P, :])
+        nc.sync.dma_start(out=w_raw[3][:], in_=wv[1][1])
         nc.sync.dma_start(out=sw[:], in_=step_weight.partition_broadcast(P))
+        nc.sync.dma_start(out=xb[3][:], in_=xv[3])
+        for i in range(S // P):
+            f_raw[i] = work.tile([P, T], BF16, tag="raw", bufs=6, name="f_raw")
+            nc.sync.dma_start(out=f_raw[i][:], in_=filters[P * i : P * (i + 1), :])
         nc.sync.dma_start(out=boot_sb[:], in_=boot.rearrange("(i p) n -> p i n", p=P))
 
         make_identity(nc, ident[:])
         make_identity(nc, ident_bf[:])
 
-        def bank(shape, dtype=F32):
-            return psum.tile(shape, dtype, tag="bank", bufs=6, name="bank")
+        def bank(shape, dtype=F32, tag="turned", bufs=2):
+            return psum.tile(shape, dtype, tag=tag, bufs=bufs, name="bank")
+
+        def head_bank(shape):
+            return bank(shape, tag="heads", bufs=4)
 
         xp = {}
         xi = {}
 
-        def x_product(g, s):
-            t = work.tile([P, K], BF16, tag="xp", bufs=4, name="xp")
-            nc.vector.tensor_tensor(out=t[:], in0=xb[g][:, s, :].bitcast(FP8), in1=scale[:], op=ALU.mult)
+        def x_cast(g, s, engine):
+            t = work.tile([P, K], BF16, tag="xp", bufs=6, name="xp")
+            source = xb[g][:, s, :].bitcast(FP8)
+            if engine == "scalar":
+                nc.scalar.copy(out=t[:], in_=source)
+            elif engine == "vector":
+                nc.vector.tensor_copy(out=t[:], in_=source)
+            else:
+                nc.gpsimd.tensor_copy(out=t[:], in_=source)
             xp[g, s] = t
+
+        def scale_columns():
+            for i in range(2):
+                nc.vector.tensor_copy(
+                    out=scale[:, :, 2 * i : 2 * i + 2, :], in_=scale_raw[:].rearrange("p q (u e) -> p q u e", e=2)
+                )
+
+        x_banks = {}
 
         def x_turn(g, h):
             for q in range(KP):
-                if h == 0:
-                    xi[g, q] = work.tile([P, 512, 4], BF16, tag="xi", bufs=4, align_bytes=64, name="xi")
-                b = bank([P, 4, P])
+                b = head_bank([P, 4, P]) if g < 2 else bank([P, 4, P], tag="acc")
                 for e in range(2):
                     words = xp[g, 2 * h + e][:].bitcast(F32)
                     for u in range(2):
                         nc.tensor.transpose(b[:, 2 * e + u, :], words[:, 256 * q + u : 256 * (q + 1) : 2], ident[:])
-                out_words = xi[g, q][:].rearrange("p c t -> p (c t)").bitcast(F32)[:, 512 * h : 512 * (h + 1)]
-                nc.scalar.copy(
-                    out=out_words.rearrange("p (c w) -> p c w", w=4), in_=b[:].rearrange("p w c -> p c w")
+                x_banks[g, h, q] = b
+
+        def x_scale_out(g, h):
+            if h == 0:
+                xi[g] = work.tile([P, KP, 512, 4], BF16, tag="xi", bufs=2, align_bytes=64, name="xi")
+            for q in range(KP):
+                part = xi[g][:, q, 2 * P * h : 2 * P * (h + 1), :].rearrange("p c t -> p (c t)")
+                nc.vector.tensor_tensor(
+                    out=part.rearrange("p (c w e) -> p c w e", w=4, e=2),
+                    in0=x_banks[g, h, q][:].bitcast(BF16).rearrange("p w (c e) -> p c w e", e=2),
+                    in1=scale[:, q, :, :].unsqueeze(1).to_broadcast([P, P, 4, 2]),
+                    op=ALU.mult,
                 )
 
         def x_quant(g):
-            for q in range(KP):
-                nc.vector.quantize_mx(
-                    out=x_codes[:, KP * g + q, :].bitcast(FP8X4),
-                    scales=x_scales[:, KP * g + q, :],
-                    in_=xi[g, q][:].rearrange("p c t -> p (c t)"),
-                )
+            both = slice(KP * g, KP * (g + 1))
+            nc.vector.quantize_mx(
+                out=x_codes[:, both, :].rearrange("p q c -> p (q c)").bitcast(FP8X4),
+                scales=x_scales[:, both, :].rearrange("p q c -> p (q c)"),
+                in_=xi[g][:].rearrange("p q c t -> p (q c t)"),
+            )
 
         wi = {}
 
         def w_interleave(i):
-            t = work.tile([P, N, 4], BF16, tag="wi", bufs=2, align_bytes=64, name="wi")
-            nc.scalar.copy(out=t[:], in_=w_raw[i][:].rearrange("p j n -> p n j"))
-            wi[i] = t
+            q, head = i // 2, i % 2
+            if head == 0:
+                wi[q] = work.tile([P, 2, N, 4], BF16, tag="wi", bufs=2, align_bytes=64, name="wi")
+            nc.scalar.copy(out=wi[q][:, head, :, :], in_=w_raw[i][:].rearrange("p j n -> p n j"))
 
-        def w_quant(i):
+        def w_quant(q):
+            both = slice(2 * q, 2 * q + 2)
             nc.vector.quantize_mx(
-                out=w_codes[:, i, :].bitcast(FP8X4),
-                scales=w_scales[:, i, :],
-                in_=wi[i][:].rearrange("p n j -> p (n j)"),
+                out=w_codes[:, both, :].rearrange("p i n -> p (i n)").bitcast(FP8X4),
+                scales=w_scales[:, both, :].rearrange("p i n -> p (i n)"),
+                in_=wi[q][:].rearrange("p i n j -> p (i n j)"),
             )
 
         f_words = f_in[:].rearrange("p g s t -> p (g s t)").bitcast(F32).rearrange("p (g s u) -> p g s u", g=G, u=2)
@@ -143,21 +172,22 @@ def tile_reward_continuation_returns_f4_kernel(
                 in_=b[:].rearrange("p (g u) s -> p g s u", u=2),
             )
 
-        def f_quant(g):
+        def f_quant(h):
+            two = slice(2 * h, 2 * h + 2)
             nc.vector.quantize_mx(
-                out=f_codes[:, g, :].bitcast(FP8X4),
-                scales=f_scales[:, g, :],
-                in_=f_in[:, g, :, :].rearrange("p s t -> p (s t)"),
+                out=f_codes[:, two, :].rearrange("p g s -> p (g s)").bitcast(FP8X4),
+                scales=f_scales[:, two, :].rearrange("p g s -> p (g s)"),
+                in_=f_in[:, two, :, :].rearrange("p g s t -> p (g s t)"),
             )
 
         zc, zr, th, e1, e2, cy, tb, cyi = {}, {}, {}, {}, {}, {}, {}, {}
         cy_codes, cy_scales = {}, {}
 
         def heads(k):
-            j, g = k // G, k % G
+            j, g = ORDER[k]
             cols = slice(P * j, P * (j + 1))
             for head, store in ((0, zc), (1, zr)):
-                b = bank([P, 512])
+                b = head_bank([P, 512])
                 for q in range(KP):
                     nc.tensor.matmul_mx(
                         out=b[:],
@@ -171,100 +201,136 @@ def tile_reward_continuation_returns_f4_kernel(
                 store[k] = b
 
         def act_tanh(k):
-            j = k // G
-            t = work.tile([P, 512], F32, tag="th", bufs=2, name="th")
+            j, g = ORDER[k]
+            t = work.tile([P, 512], F32, tag="th", bufs=3, name="th")
             nc.scalar.activation(out=t[:], in_=zc[k][:], func=ACT.Tanh, bias=bias[:, J + j : J + j + 1], scale=0.5)
             th[k] = t
 
-        def act_exp(k):
-            j = k // G
+        def act_exp_minus(k):
+            j, g = ORDER[k]
             t = work.tile([P, 512], F32, tag="e2", bufs=3, name="e2")
             nc.scalar.activation(out=t[:], in_=zr[k][:], func=ACT.Exp, bias=bias[:, 2 * J + j : 2 * J + j + 1], scale=-1.0)
             e2[k] = t
+
+        def act_exp_plus(k):
+            j, g = ORDER[k]
             t = work.tile([P, 512], F32, tag="e1", bufs=3, name="e1")
             nc.scalar.activation(out=t[:], in_=zr[k][:], func=ACT.Exp, bias=bias[:, j : j + 1], scale=1.0)
             e1[k] = t
 
-        def epilogue(k):
-            g = k % G
-            e2m = work.tile([P, 512], F32, tag="e2m", bufs=2, name="e2m")
-            nc.vector.tensor_scalar(out=e2m[:], in0=e2[k][:], scalar1=1.0, scalar2=None, op0=ALU.max)
-            c2 = work.tile([P, 512], F32, tag="c2", bufs=2, name="c2")
-            nc.vector.scalar_tensor_tensor(
-                out=c2[:], in0=th[k][:], scalar=1.0, in1=sw_cols[:, 512 * g : 512 * (g + 1)], op0=ALU.add, op1=ALU.mult
-            )
-            dd = work.tile([P, 512], F32, tag="dd", bufs=2, name="dd")
-            nc.vector.scalar_tensor_tensor(
-                out=dd[:], in0=e1[k][:], scalar=1.0, in1=e2m[:], op0=ALU.max, op1=ALU.subtract
-            )
-            t = work.tile([P, 2, 512], BF16, tag="cy", bufs=3, name="cy")
-            nc.vector.tensor_scalar(out=t[:, 0, :], in0=c2[:], scalar1=0.5, scalar2=None, op0=ALU.mult)
-            nc.vector.scalar_tensor_tensor(
-                out=t[:, 1, :], in0=c2[:], scalar=0.5, in1=dd[:], op0=ALU.mult, op1=ALU.mult
-            )
-            cy[k] = t
+        c2 = {}
 
-        def turn(k):
-            words = cy[k][:].rearrange("p i c -> p (i c)").bitcast(F32)
-            b = bank([P, 4, P])
-            for w in range(4):
-                nc.tensor.transpose(b[:, w, :], words[:, P * w : P * (w + 1)], ident[:])
-            tb[k] = b
+        def ep_c(k):
+            j, g = ORDER[k]
+            c2[k] = work.tile([P, 512], F32, tag="c2", bufs=2, name="c2")
+            weights = sw[:, 512 * g : 512 * (g + 1)].rearrange("p (c h e) -> p h c e", h=2, e=2)
+            for h in range(2):
+                half = slice(256 * h, 256 * (h + 1))
+                nc.vector.scalar_tensor_tensor(
+                    out=c2[k][:, half].rearrange("p (c e) -> p c e", e=2),
+                    in0=th[k][:, half].rearrange("p (c e) -> p c e", e=2),
+                    scalar=1.0,
+                    in1=weights[:, h, :, :],
+                    op0=ALU.add,
+                    op1=ALU.mult,
+                )
 
-        def turn_out(k):
-            t = work.tile([P, 2, P, 4], BF16, tag="cyi", bufs=3, align_bytes=64, name="cyi")
-            out_words = t[:].rearrange("p i n t -> p (i n t)").bitcast(F32)
+        def ep_cast(k):
+            cy[k] = work.tile([P, 2, 512], BF16, tag="cy", bufs=3, name="cy")
+            if k in CAST_ON_SCALAR:
+                nc.scalar.activation(out=cy[k][:, 0, :], in_=c2[k][:], func=ACT.Copy, scale=0.5)
+            else:
+                nc.vector.tensor_scalar(out=cy[k][:, 0, :], in0=c2[k][:], scalar1=0.5, scalar2=None, op0=ALU.mult)
+
+        def ep_floor(k):
+            nc.vector.tensor_scalar(out=e2[k][:], in0=e2[k][:], scalar1=1.0, scalar2=None, op0=ALU.max)
+
+        def ep_symexp(k):
+            nc.vector.scalar_tensor_tensor(
+                out=e1[k][:], in0=e1[k][:], scalar=1.0, in1=e2[k][:], op0=ALU.max, op1=ALU.subtract
+            )
+
+        def ep_y(k):
+            nc.vector.scalar_tensor_tensor(
+                out=cy[k][:, 1, :], in0=c2[k][:], scalar=0.5, in1=e1[k][:], op0=ALU.mult, op1=ALU.mult
+            )
+
+        def turn(k, kinds):
+            b = bank([P, len(kinds), 2, P])
+            for n, kind in enumerate(kinds):
+                words = cy[k][:, kind, :].bitcast(F32)
+                for h in range(2):
+                    nc.tensor.transpose(b[:, n, h, :], words[:, P * h : P * (h + 1)], ident[:])
+            tb[k, kinds[0]] = b
+
+        def turn_out(k, kinds):
+            if kinds[0] == 0:
+                cyi[k] = work.tile([P, 2, P, 4], BF16, tag="cyi", bufs=3, align_bytes=64, name="cyi")
+            part = cyi[k][:, kinds[0] : kinds[0] + len(kinds), :, :]
             nc.scalar.copy(
-                out=out_words.rearrange("p (i n h) -> p i n h", i=2, h=2),
-                in_=tb[k][:].rearrange("p (i h) n -> p i n h", h=2),
+                out=part.rearrange("p w n t -> p (w n t)").bitcast(F32).rearrange("p (w n h) -> p w n h", n=P, h=2),
+                in_=tb[k, kinds[0]][:].rearrange("p w h n -> p w n h"),
             )
-            cyi[k] = t
 
-        def turn_quant(k):
-            j, g = k // G, k % G
+        def turn_quant(k, kinds):
+            j, g = ORDER[k]
             if g == 0:
-                cy_codes[j] = work.tile([P, G, 2 * P], U32, tag="cy_codes", bufs=2, align_bytes=64, name="cy_codes")
-                cy_scales[j] = work.tile([P, G, 2 * P], U8, tag="cy_scales", bufs=2, align_bytes=64, name="cy_scales")
+                cy_codes[j] = work.tile([P, G, 2 * P], U32, tag="cy_codes", bufs=3, align_bytes=64, name="cy_codes")
+                cy_scales[j] = work.tile([P, G, 2 * P], U8, tag="cy_scales", bufs=3, align_bytes=64, name="cy_scales")
+            cols = slice(P * kinds[0], P * (kinds[0] + len(kinds)))
             nc.vector.quantize_mx(
-                out=cy_codes[j][:, g, :].bitcast(FP8X4),
-                scales=cy_scales[j][:, g, :],
-                in_=cyi[k][:].rearrange("p i n t -> p (i n t)"),
+                out=cy_codes[j][:, g, cols].bitcast(FP8X4),
+                scales=cy_scales[j][:, g, cols],
+                in_=cyi[k][:, kinds[0] : kinds[0] + len(kinds), :, :].rearrange("p w n t -> p (w n t)"),
             )
 
         acc = {}
 
-        def filter_pass(j, i, g, out):
+        def filter_pass(j, i, g, out, cols):
             nc.tensor.matmul_mx(
                 out=out,
                 lhsT=f_codes[:, g, P * i : P * (i + 1)].bitcast(FP8X4),
                 lhsT_scale=f_scales[:, g, P * i : P * (i + 1)],
-                rhs=cy_codes[j][:, g, :].bitcast(FP8X4),
-                rhs_scale=cy_scales[j][:, g, :],
+                rhs=cy_codes[j][:, g, cols].bitcast(FP8X4),
+                rhs_scale=cy_scales[j][:, g, cols],
                 start=(g == 0),
                 stop=(g == G - 1),
             )
 
         def filter_sums(j, i):
             if i % 2 == 0:
-                acc[j, i // 2] = psum.tile([P, 2, 2 * P], F32, tag="acc", bufs=2, name="acc")
+                acc[j, i // 2] = bank([P, 2, 2 * P], tag="acc")
             for g in range(G):
-                filter_pass(j, i, g, acc[j, i // 2][:, i % 2, :])
+                filter_pass(j, i, g, acc[j, i // 2][:, i % 2, :], slice(0, 2 * P))
 
         mass_out = out_1.rearrange("(i p) n -> p i n", p=P)
         ret_out = out_0.rearrange("(i p) n -> p i n", p=P)
+        t2 = {}
 
-        def finish(j, rows, a):
-            n = rows.stop - rows.start
-            cols = slice(P * j, P * (j + 1))
-            ms = work.tile([P, n, P], F32, tag="ms%d" % n, bufs=2, name="ms")
+        t1s = {}
+
+        def finish_product(j, h):
+            rows, cols = slice(2 * h, 2 * h + 2), slice(P * j, P * (j + 1))
+            a = acc[j, h][:]
+            ms = work.tile([P, 2, P], F32, tag="ms", bufs=2, name="ms")
             nc.scalar.copy(out=ms[:], in_=a[:, :, 0:P])
             nc.sync.dma_start(out=mass_out[:, rows, cols], in_=ms[:])
-            t1 = work.tile([P, n, P], F32, tag="t1%d" % n, bufs=2, name="t1")
+            t1 = work.tile([P, 2, P], F32, tag="t1", bufs=2, name="t1")
             nc.vector.tensor_tensor(out=t1[:], in0=a[:, :, 0:P], in1=boot_sb[:, rows, cols], op=ALU.mult)
-            t2 = work.tile([P, n, P], F32, tag="t2%d" % n, bufs=2, name="t2")
-            nc.vector.tensor_tensor(out=t2[:], in0=a[:, :, P : 2 * P], in1=t1[:], op=ALU.add)
-            nc.scalar.activation(out=log_sb[:, rows, cols], in_=t2[:], func=ACT.Abs)
-            nc.scalar.activation(out=sign_sb[:, rows, cols], in_=t2[:], func=ACT.Sign)
+            t1s[j, h] = t1
+
+        def finish_add(j, h):
+            rows, cols = slice(2 * h, 2 * h + 2), slice(P * j, P * (j + 1))
+            a = acc[j, h][:]
+            t1 = t1s[j, h]
+            if h == 0:
+                t2[j] = work.tile([P, 4, P], F32, tag="t2", bufs=2, name="t2")
+            nc.vector.tensor_tensor(out=t2[j][:, rows, :], in0=a[:, :, P : 2 * P], in1=t1[:], op=ALU.add)
+
+        def finish_abs(j, rows):
+            cols = slice(P * j, P * (j + 1))
+            nc.scalar.activation(out=log_sb[:, rows, cols], in_=t2[j][:, rows, :], func=ACT.Abs)
+            nc.scalar.activation(out=sign_sb[:, rows, cols], in_=t2[j][:, rows, :], func=ACT.Sign)
 
         def symlog(rows, cols):
             nc.scalar.activation(out=log_sb[:, rows, cols], in_=log_sb[:, rows, cols], func=ACT.Ln, bias=1.0, scale=1.0)
@@ -275,93 +341,149 @@ def tile_reward_continuation_returns_f4_kernel(
             )
             nc.sync.dma_start(out=ret_out[:, rows, cols], in_=log_sb[:, rows, cols])
 
-        for g in range(G):
-            x_product(g, 0)
-            x_product(g, 1)
-            if g == 0:
-                w_interleave(0)
-            x_turn(g, 0)
-            if g == 0:
-                w_interleave(1)
-            if g == 1:
-                w_interleave(2)
-            x_product(g, 2)
-            x_product(g, 3)
-            x_turn(g, 1)
-            if g == 1:
-                w_quant(0)
-                w_quant(1)
-                w_interleave(3)
-            if g == 2:
-                w_quant(2)
-                b_t = bank([P, P], BF16)
-                nc.tensor.transpose(b_t[:], b_rows[:], ident_bf[:])
-                nc.vector.tensor_scalar(out=bias[:, 0:J], in0=b_t[:, 0:J], scalar1=1.0, scalar2=None, op0=ALU.mult)
+        def bias_columns():
+            b_t = bank([P, P], BF16)
+            nc.tensor.transpose(b_t[:], b_rows[:], ident_bf[:])
+            for first, source, factor in ((0, 0, 1.0), (J, J, 0.5), (2 * J, 0, -1.0)):
                 nc.vector.tensor_scalar(
-                    out=bias[:, J : 2 * J], in0=b_t[:, J : 2 * J], scalar1=0.5, scalar2=None, op0=ALU.mult
+                    out=bias[:, first : first + J], in0=b_t[:, source : source + J], scalar1=factor, scalar2=None, op0=ALU.mult
                 )
-                nc.vector.tensor_scalar(
-                    out=bias[:, 2 * J : 3 * J], in0=b_t[:, 0:J], scalar1=-1.0, scalar2=None, op0=ALU.mult
-                )
-                w_quant(3)
-            if g > 0:
-                x_quant(g - 1)
-            if g >= 2:
-                for i in (2 * g - 4, 2 * g - 3):
-                    f_turn(i, 0)
-                    f_turn(i, 1)
-            if g == 3:
-                nc.scalar.copy(
-                    out=sw_cols[:].bitcast(F32).rearrange("p (g h c) -> p g h c", g=G, h=2),
-                    in_=sw[:].bitcast(F32).rearrange("p (g c h) -> p g h c", g=G, h=2),
-                )
+
+        def act_unit(k):
+            act_tanh(k)
+            act_exp_minus(k)
+            act_exp_plus(k)
+
+        def turn_f(i):
+            f_turn(i, 0)
+            f_turn(i, 1)
+
+        for s in range(4):
+            x_cast(0, s, ("vector", "vector", "vector", "scalar")[s])
+            if s == 1:
+                scale_columns()
+                x_turn(0, 0)
+        x_scale_out(0, 0)
+        x_turn(0, 1)
+        x_scale_out(0, 1)
+        for g in range(1, G):
+            for s in range(4):
+                x_cast(g, s, "gpsimd")
+        w_interleave(0)
+        w_interleave(1)
+        x_turn(1, 0)
+        x_scale_out(1, 0)
+        x_quant(0)
+        x_turn(1, 1)
+        x_scale_out(1, 1)
+        w_quant(0)
+        w_interleave(2)
+        w_interleave(3)
+        bias_columns()
+        w_quant(1)
+        x_turn(2, 0)
+        turn_f(0)
         heads(0)
+        x_scale_out(2, 0)
+        x_turn(2, 1)
+        x_quant(1)
+        act_unit(0)
+        turn_f(1)
+        x_scale_out(2, 1)
         heads(1)
-        act_tanh(0)
-        act_exp(0)
-        x_quant(G - 1)
-        for g in range(G):
-            f_quant(g)
+        x_turn(3, 0)
 
         all_rows = slice(0, S // P)
+        both = (0, 1)
         tail = {}
-        for k in range(UNITS + 1):
-            if 1 <= k:
-                turn(k - 1)
+        last = UNITS - 1
+        for k in range(last):
+            if k >= 1:
+                turn(k - 1, both)
             if k + 2 < UNITS:
                 heads(k + 2)
-            if k + 1 < UNITS:
-                act_tanh(k + 1)
-            if 1 <= k:
-                turn_out(k - 1)
-            if k + 1 < UNITS:
-                act_exp(k + 1)
-            if k < UNITS:
-                epilogue(k)
-            if 1 <= k:
-                turn_quant(k - 1)
-            if k <= 12 and k >= 5:
-                j, i = (k - 5) // 4, (k - 5) % 4
+            act_tanh(k + 1)
+            act_exp_minus(k + 1)
+            ep_floor(k)
+            ep_c(k)
+            ep_symexp(k)
+            if k in FINISH:
+                finish_product(*FINISH[k])
+            if k >= 1:
+                turn_out(k - 1, both)
+            ep_cast(k)
+            act_exp_plus(k + 1)
+            if k in (0, 1):
+                x_scale_out(3, k)
+            if k in (4, 5):
+                f_quant(k - 4)
+            if k >= 1:
+                turn_quant(k - 1, both)
+            ep_y(k)
+            if k == 0:
+                x_turn(3, 1)
+            if k in (0, 1):
+                turn_f(k + 2)
+            if k == 0:
+                x_quant(2)
+            if k == 2:
+                x_quant(3)
+            if k in FINISH:
+                finish_add(*FINISH[k])
+            if k in SUMS:
+                j, i = SUMS[k]
                 filter_sums(j, i)
-                if i % 2 == 1:
-                    finish(j, slice(i - 1, i + 1), acc[j, i // 2][:])
-            if k == 13 or k == 14:
-                i = 2 * (k - 13)
-                filter_sums(2, i)
-                filter_sums(2, i + 1)
-                finish(2, slice(i, i + 2), acc[2, i // 2][:])
-            if k == 15:
-                for i in range(S // P):
-                    tail[i] = bank([P, 1, 2 * P])
-                    filter_pass(3, i, 0, tail[i][:, 0, :])
-                    filter_pass(3, i, 1, tail[i][:, 0, :])
-                symlog(all_rows, slice(0, 3 * P))
-            if k == 16:
-                for i in range(S // P):
-                    filter_pass(3, i, 2, tail[i][:, 0, :])
-                symlog_store(all_rows, slice(0, 3 * P))
-                for i in range(S // P):
-                    filter_pass(3, i, 3, tail[i][:, 0, :])
-                    finish(3, slice(i, i + 1), tail[i][:])
-                symlog(all_rows, slice(3 * P, 4 * P))
-                symlog_store(all_rows, slice(3 * P, 4 * P))
+                filter_sums(j, i + 1)
+            if k in (10, 12):
+                finish_abs((k - 10) // 2, all_rows)
+        turn(last - 1, both)
+        turn_out(last - 1, both)
+        ep_c(last)
+        finish_product(2, 1)
+        ep_floor(last)
+        ep_cast(last)
+        turn(last, (0,))
+        turn_out(last, (0,))
+        ep_symexp(last)
+        turn_quant(last - 1, both)
+        finish_add(2, 1)
+        ep_y(last)
+        for i in range(S // P):
+            tail[i] = head_bank([P, P])
+            for g in range(2):
+                filter_pass(3, i, g, tail[i][:], slice(P, 2 * P))
+        turn(last, (1,))
+        finish_abs(2, all_rows)
+        turn_out(last, (1,))
+        symlog(all_rows, slice(0, 2 * P))
+        turn_quant(last, (0,))
+        for i in range(S // P):
+            filter_pass(3, i, 2, tail[i][:], slice(P, 2 * P))
+        mass = bank([P, 4, P])
+        for i in range(S // P):
+            for g in range(G):
+                filter_pass(3, i, g, mass[:, i, :], slice(0, P))
+        turn_quant(last, (1,))
+        for i in range(S // P):
+            filter_pass(3, i, 3, tail[i][:], slice(P, 2 * P))
+        cols = slice(3 * P, 4 * P)
+        t1 = work.tile([P, 4, P], F32, tag="t1", bufs=2, name="t1")
+        nc.vector.tensor_tensor(out=t1[:], in0=mass[:], in1=boot_sb[:, :, cols], op=ALU.mult)
+        ms = work.tile([P, 4, P], F32, tag="ms", bufs=2, name="ms")
+        t2[3] = work.tile([P, 4, P], F32, tag="t2", bufs=2, name="t2")
+        for i in range(S // P):
+            nc.vector.tensor_tensor(out=t2[3][:, i, :], in0=tail[i][:], in1=t1[:, i, :], op=ALU.add)
+        symlog_store(all_rows, slice(0, 2 * P))
+        nc.scalar.activation(out=log_sb[:, :, cols], in_=t2[3][:], func=ACT.Abs)
+        symlog(all_rows, cols)
+        nc.vector.tensor_scalar(
+            out=sign_sb[:, :, cols], in0=t2[3][:], scalar1=0.0, scalar2=2.0, op0=ALU.is_ge, op1=ALU.mult
+        )
+        nc.vector.scalar_tensor_tensor(
+            out=log_sb[:, :, cols], in0=sign_sb[:, :, cols], scalar=-1.0, in1=log_sb[:, :, cols], op0=ALU.add, op1=ALU.mult
+        )
+        nc.sync.dma_start(out=ret_out[:, :, cols], in_=log_sb[:, :, cols])
+        symlog(all_rows, slice(2 * P, 3 * P))
+        symlog_store(all_rows, slice(2 * P, 3 * P))
+        nc.scalar.copy(out=ms[:], in_=mass[:])
+        nc.sync.dma_start(out=mass_out[:, :, cols], in_=ms[:])

@@ -21,7 +21,11 @@ UNITS = J * G
 ORDER = [(j, 2 * half + i) for half in range(2) for j in range(2) for i in range(2)] + [(j, g) for j in (2, 3) for g in range(G)]
 SUMS = {7: (0, 0), 8: (0, 2), 9: (1, 0), 10: (1, 2), 13: (2, 0), 14: (2, 2)}
 FINISH = {8: (0, 0), 9: (0, 1), 10: (1, 0), 11: (1, 1), 14: (2, 0)}
-CAST_ON_SCALAR = tuple(range(6))
+FLOOR_ON_SCALAR = ()
+LAST_X = (0, 1)
+FILTER_QUANT = (4, 5)
+FILTER_TURN = (0, 1)
+CAST_ON_SCALAR = (0, 2, 3, 4, 5, 6, 8, 14)
 
 FLOPS = 2 * T * K * 2 * N + 2 * S * T * 2 * N
 
@@ -43,6 +47,7 @@ def tile_reward_continuation_returns_f4_kernel(
         scale_raw = keep.tile([P, KP, 4], F32)
         scale = keep.tile([P, KP, 4, 2], F32)
         sw = keep.tile([P, T], BF16)
+        sw_cols = keep.tile([P, T], BF16)
         boot_sb = keep.tile([P, S // P, N], BF16)
         xb = [keep.tile([P, 4, K], U8, name="xb%d" % g) for g in range(G)]
         w_raw = [work.tile([P, 4, N], BF16, tag="raw", bufs=6, name="w_raw") for i in range(2 * KP)]
@@ -206,11 +211,22 @@ def tile_reward_continuation_returns_f4_kernel(
             nc.scalar.activation(out=t[:], in_=zc[k][:], func=ACT.Tanh, bias=bias[:, J + j : J + j + 1], scale=0.5)
             th[k] = t
 
+        def act_unit_start(k):
+            j, g = ORDER[k]
+            e2[k] = work.tile([P, 512], F32, tag="e2", bufs=3, name="e2")
+            if k in FLOOR_ON_SCALAR:
+                nc.scalar.activation(
+                    out=e2[k][:], in_=zr[k][:], func=ACT.Relu, bias=bias[:, 2 * J + j : 2 * J + j + 1], scale=-1.0
+                )
+            act_tanh(k)
+            act_exp_minus(k)
+
         def act_exp_minus(k):
             j, g = ORDER[k]
-            t = work.tile([P, 512], F32, tag="e2", bufs=3, name="e2")
-            nc.scalar.activation(out=t[:], in_=zr[k][:], func=ACT.Exp, bias=bias[:, 2 * J + j : 2 * J + j + 1], scale=-1.0)
-            e2[k] = t
+            source, offset, factor = zr[k], bias[:, 2 * J + j : 2 * J + j + 1], -1.0
+            if k in FLOOR_ON_SCALAR:
+                source, offset, factor = e2[k], 0.0, 1.0
+            nc.scalar.activation(out=e2[k][:], in_=source[:], func=ACT.Exp, bias=offset, scale=factor)
 
         def act_exp_plus(k):
             j, g = ORDER[k]
@@ -223,17 +239,9 @@ def tile_reward_continuation_returns_f4_kernel(
         def ep_c(k):
             j, g = ORDER[k]
             c2[k] = work.tile([P, 512], F32, tag="c2", bufs=2, name="c2")
-            weights = sw[:, 512 * g : 512 * (g + 1)].rearrange("p (c h e) -> p h c e", h=2, e=2)
-            for h in range(2):
-                half = slice(256 * h, 256 * (h + 1))
-                nc.vector.scalar_tensor_tensor(
-                    out=c2[k][:, half].rearrange("p (c e) -> p c e", e=2),
-                    in0=th[k][:, half].rearrange("p (c e) -> p c e", e=2),
-                    scalar=1.0,
-                    in1=weights[:, h, :, :],
-                    op0=ALU.add,
-                    op1=ALU.mult,
-                )
+            nc.vector.scalar_tensor_tensor(
+                out=c2[k][:], in0=th[k][:], scalar=1.0, in1=sw_cols[:, 512 * g : 512 * (g + 1)], op0=ALU.add, op1=ALU.mult
+            )
 
         def ep_cast(k):
             cy[k] = work.tile([P, 2, 512], BF16, tag="cy", bufs=3, name="cy")
@@ -243,7 +251,8 @@ def tile_reward_continuation_returns_f4_kernel(
                 nc.vector.tensor_scalar(out=cy[k][:, 0, :], in0=c2[k][:], scalar1=0.5, scalar2=None, op0=ALU.mult)
 
         def ep_floor(k):
-            nc.vector.tensor_scalar(out=e2[k][:], in0=e2[k][:], scalar1=1.0, scalar2=None, op0=ALU.max)
+            if k not in FLOOR_ON_SCALAR:
+                nc.vector.tensor_scalar(out=e2[k][:], in0=e2[k][:], scalar1=1.0, scalar2=None, op0=ALU.max)
 
         def ep_symexp(k):
             nc.vector.scalar_tensor_tensor(
@@ -327,19 +336,37 @@ def tile_reward_continuation_returns_f4_kernel(
                 t2[j] = work.tile([P, 4, P], F32, tag="t2", bufs=2, name="t2")
             nc.vector.tensor_tensor(out=t2[j][:, rows, :], in0=a[:, :, P : 2 * P], in1=t1[:], op=ALU.add)
 
-        def finish_abs(j, rows):
+        def finish_abs(j):
             cols = slice(P * j, P * (j + 1))
-            nc.scalar.activation(out=log_sb[:, rows, cols], in_=t2[j][:, rows, :], func=ACT.Abs)
-            nc.scalar.activation(out=sign_sb[:, rows, cols], in_=t2[j][:, rows, :], func=ACT.Sign)
+            nc.scalar.activation(out=log_sb[:, :, cols], in_=t2[j][:], func=ACT.Abs)
+
+        def finish_sign(j):
+            cols = slice(P * j, P * (j + 1))
+            if j < 2:
+                nc.scalar.activation(out=sign_sb[:, :, cols], in_=t2[j][:], func=ACT.Sign)
+            else:
+                nc.vector.tensor_scalar(
+                    out=sign_sb[:, :, cols], in0=t2[j][:], scalar1=0.0, scalar2=2.0, op0=ALU.is_ge, op1=ALU.mult
+                )
 
         def symlog(rows, cols):
             nc.scalar.activation(out=log_sb[:, rows, cols], in_=log_sb[:, rows, cols], func=ACT.Ln, bias=1.0, scale=1.0)
 
-        def symlog_store(rows, cols):
-            nc.vector.tensor_tensor(
-                out=log_sb[:, rows, cols], in0=log_sb[:, rows, cols], in1=sign_sb[:, rows, cols], op=ALU.mult
-            )
-            nc.sync.dma_start(out=ret_out[:, rows, cols], in_=log_sb[:, rows, cols])
+        def symlog_store(j, cols):
+            if j < 2:
+                nc.vector.tensor_tensor(
+                    out=log_sb[:, :, cols], in0=log_sb[:, :, cols], in1=sign_sb[:, :, cols], op=ALU.mult
+                )
+            else:
+                nc.vector.scalar_tensor_tensor(
+                    out=log_sb[:, :, cols],
+                    in0=sign_sb[:, :, cols],
+                    scalar=-1.0,
+                    in1=log_sb[:, :, cols],
+                    op0=ALU.add,
+                    op1=ALU.mult,
+                )
+            nc.sync.dma_start(out=ret_out[:, :, cols], in_=log_sb[:, :, cols])
 
         def bias_columns():
             b_t = bank([P, P], BF16)
@@ -350,8 +377,7 @@ def tile_reward_continuation_returns_f4_kernel(
                 )
 
         def act_unit(k):
-            act_tanh(k)
-            act_exp_minus(k)
+            act_unit_start(k)
             act_exp_plus(k)
 
         def turn_f(i):
@@ -369,6 +395,10 @@ def tile_reward_continuation_returns_f4_kernel(
         for g in range(1, G):
             for s in range(4):
                 x_cast(g, s, "gpsimd")
+        nc.gpsimd.tensor_copy(
+            out=sw_cols[:].bitcast(F32).rearrange("p (g h c) -> p g h c", g=G, h=2),
+            in_=sw[:].bitcast(F32).rearrange("p (g c h) -> p g h c", g=G, h=2),
+        )
         w_interleave(0)
         w_interleave(1)
         x_turn(1, 0)
@@ -402,8 +432,7 @@ def tile_reward_continuation_returns_f4_kernel(
                 turn(k - 1, both)
             if k + 2 < UNITS:
                 heads(k + 2)
-            act_tanh(k + 1)
-            act_exp_minus(k + 1)
+            act_unit_start(k + 1)
             ep_floor(k)
             ep_c(k)
             ep_symexp(k)
@@ -413,17 +442,17 @@ def tile_reward_continuation_returns_f4_kernel(
                 turn_out(k - 1, both)
             ep_cast(k)
             act_exp_plus(k + 1)
-            if k in (0, 1):
-                x_scale_out(3, k)
-            if k in (4, 5):
-                f_quant(k - 4)
+            if k in LAST_X:
+                x_scale_out(3, LAST_X.index(k))
+            if k in FILTER_QUANT:
+                f_quant(FILTER_QUANT.index(k))
             if k >= 1:
                 turn_quant(k - 1, both)
             ep_y(k)
-            if k == 0:
+            if k == LAST_X[1] - 1:
                 x_turn(3, 1)
-            if k in (0, 1):
-                turn_f(k + 2)
+            if k in FILTER_TURN:
+                turn_f(2 + FILTER_TURN.index(k))
             if k == 0:
                 x_quant(2)
             if k == 2:
@@ -435,55 +464,52 @@ def tile_reward_continuation_returns_f4_kernel(
                 filter_sums(j, i)
                 filter_sums(j, i + 1)
             if k in (10, 12):
-                finish_abs((k - 10) // 2, all_rows)
+                finish_abs((k - 10) // 2)
+                finish_sign((k - 10) // 2)
         turn(last - 1, both)
         turn_out(last - 1, both)
         ep_c(last)
-        finish_product(2, 1)
         ep_floor(last)
         ep_cast(last)
         turn(last, (0,))
         turn_out(last, (0,))
+        finish_product(2, 1)
         ep_symexp(last)
         turn_quant(last - 1, both)
         finish_add(2, 1)
-        ep_y(last)
         for i in range(S // P):
             tail[i] = head_bank([P, P])
-            for g in range(2):
+        for g in range(3):
+            for i in range(S // P):
                 filter_pass(3, i, g, tail[i][:], slice(P, 2 * P))
-        turn(last, (1,))
-        finish_abs(2, all_rows)
-        turn_out(last, (1,))
-        symlog(all_rows, slice(0, 2 * P))
         turn_quant(last, (0,))
-        for i in range(S // P):
-            filter_pass(3, i, 2, tail[i][:], slice(P, 2 * P))
+        ep_y(last)
+        nc.scalar.activation(out=warm[:], in_=warm[:], func=ACT.Ln, bias=1.0)
         mass = bank([P, 4, P])
         for i in range(S // P):
+            if i == 2:
+                turn(last, (1,))
             for g in range(G):
                 filter_pass(3, i, g, mass[:, i, :], slice(0, P))
-        turn_quant(last, (1,))
-        for i in range(S // P):
-            filter_pass(3, i, 3, tail[i][:], slice(P, 2 * P))
+        turn_out(last, (1,))
         cols = slice(3 * P, 4 * P)
         t1 = work.tile([P, 4, P], F32, tag="t1", bufs=2, name="t1")
-        nc.vector.tensor_tensor(out=t1[:], in0=mass[:], in1=boot_sb[:, :, cols], op=ALU.mult)
         ms = work.tile([P, 4, P], F32, tag="ms", bufs=2, name="ms")
         t2[3] = work.tile([P, 4, P], F32, tag="t2", bufs=2, name="t2")
+        finish_sign(2)
+        turn_quant(last, (1,))
+        nc.vector.tensor_tensor(out=t1[:], in0=mass[:], in1=boot_sb[:, :, cols], op=ALU.mult)
+        finish_abs(2)
+        symlog(all_rows, slice(0, 3 * P))
+        for i in range(S // P):
+            filter_pass(3, i, 3, tail[i][:], slice(P, 2 * P))
+        nc.vector.tensor_copy(out=ms[:], in_=mass[:])
+        nc.sync.dma_start(out=mass_out[:, :, cols], in_=ms[:])
         for i in range(S // P):
             nc.vector.tensor_tensor(out=t2[3][:, i, :], in0=tail[i][:], in1=t1[:, i, :], op=ALU.add)
-        symlog_store(all_rows, slice(0, 2 * P))
-        nc.scalar.activation(out=log_sb[:, :, cols], in_=t2[3][:], func=ACT.Abs)
+        finish_abs(3)
         symlog(all_rows, cols)
-        nc.vector.tensor_scalar(
-            out=sign_sb[:, :, cols], in0=t2[3][:], scalar1=0.0, scalar2=2.0, op0=ALU.is_ge, op1=ALU.mult
-        )
-        nc.vector.scalar_tensor_tensor(
-            out=log_sb[:, :, cols], in0=sign_sb[:, :, cols], scalar=-1.0, in1=log_sb[:, :, cols], op0=ALU.add, op1=ALU.mult
-        )
-        nc.sync.dma_start(out=ret_out[:, :, cols], in_=log_sb[:, :, cols])
-        symlog(all_rows, slice(2 * P, 3 * P))
-        symlog_store(all_rows, slice(2 * P, 3 * P))
-        nc.scalar.copy(out=ms[:], in_=mass[:])
-        nc.sync.dma_start(out=mass_out[:, :, cols], in_=ms[:])
+        finish_sign(3)
+        symlog_store(0, slice(0, 2 * P))
+        symlog_store(2, slice(2 * P, 3 * P))
+        symlog_store(3, cols)

@@ -23,9 +23,9 @@ SUMS = {7: (0, 0), 8: (0, 2), 9: (1, 0), 10: (1, 2), 13: (2, 0), 14: (2, 2)}
 FINISH = {8: (0, 0), 9: (0, 1), 10: (1, 0), 11: (1, 1), 14: (2, 0)}
 FLOOR_ON_SCALAR = ()
 LAST_X = (0, 1)
-FILTER_QUANT = (4, 5)
-FILTER_TURN = (0, 1)
-CAST_ON_SCALAR = (0, 2, 3, 4, 5, 6, 8, 14)
+FILTER_QUANT = (3, 5)
+FILTER_TURN = (1, 2)
+CAST_ON_SCALAR = (1, 2, 3, 4, 5, 6, 8, 14)
 
 FLOPS = 2 * T * K * 2 * N + 2 * S * T * 2 * N
 
@@ -47,7 +47,6 @@ def tile_reward_continuation_returns_f4_kernel(
         scale_raw = keep.tile([P, KP, 4], F32)
         scale = keep.tile([P, KP, 4, 2], F32)
         sw = keep.tile([P, T], BF16)
-        sw_cols = keep.tile([P, T], BF16)
         boot_sb = keep.tile([P, S // P, N], BF16)
         xb = [keep.tile([P, 4, K], U8, name="xb%d" % g) for g in range(G)]
         w_raw = [work.tile([P, 4, N], BF16, tag="raw", bufs=6, name="w_raw") for i in range(2 * KP)]
@@ -70,22 +69,42 @@ def tile_reward_continuation_returns_f4_kernel(
         nc.vector.memset(warm[:], 0.0)
         nc.scalar.dma_start(out=scale_raw[:], in_=x_scale.rearrange("o (q p t) -> p (o q) t", p=P, t=4))
         nc.scalar.activation(out=warm[:], in_=warm[:], func=ACT.Exp)
-        nc.sync.dma_start(out=xb[0][:, 0:2, :], in_=xv[0][:, 0:2, :])
-        nc.sync.dma_start(out=xb[0][:, 2:4, :], in_=xv[0][:, 2:4, :])
-        nc.sync.dma_start(out=w_raw[0][:], in_=wv[0][0])
-        nc.sync.dma_start(out=xb[1][:], in_=xv[1])
-        nc.sync.dma_start(out=w_raw[1][:], in_=wv[1][0])
-        nc.sync.dma_start(out=b_rows[0:4, :], in_=b_reward.rearrange("(c p) -> c p", p=P))
-        nc.sync.dma_start(out=b_rows[4:8, :], in_=b_cont.rearrange("(c p) -> c p", p=P))
-        nc.sync.dma_start(out=w_raw[2][:], in_=wv[0][1])
-        nc.sync.dma_start(out=xb[2][:], in_=xv[2])
-        nc.sync.dma_start(out=w_raw[3][:], in_=wv[1][1])
-        nc.sync.dma_start(out=sw[:], in_=step_weight.partition_broadcast(P))
-        nc.sync.dma_start(out=xb[3][:], in_=xv[3])
-        for i in range(S // P):
+        def load_x(g, first, last):
+            nc.sync.dma_start(out=xb[g][:, first:last, :], in_=xv[g][:, first:last, :])
+
+        def load_w(i):
+            nc.sync.dma_start(out=w_raw[i][:], in_=wv[i % 2][i // 2])
+
+        def load_f(i):
             f_raw[i] = work.tile([P, T], BF16, tag="raw", bufs=6, name="f_raw")
             nc.sync.dma_start(out=f_raw[i][:], in_=filters[P * i : P * (i + 1), :])
-        nc.sync.dma_start(out=boot_sb[:], in_=boot.rearrange("(i p) n -> p i n", p=P))
+
+        def load_biases():
+            nc.sync.dma_start(out=b_rows[0:4, :], in_=b_reward.rearrange("(c p) -> c p", p=P))
+            nc.sync.dma_start(out=b_rows[4:8, :], in_=b_cont.rearrange("(c p) -> c p", p=P))
+
+        def load_sw():
+            nc.sync.dma_start(out=sw[:], in_=step_weight.partition_broadcast(P))
+
+        def load_boot():
+            nc.sync.dma_start(out=boot_sb[:], in_=boot.rearrange("(i p) n -> p i n", p=P))
+
+        load_x(0, 0, 2)
+        load_x(0, 2, 4)
+        load_x(1, 0, 4)
+        load_w(0)
+        load_w(1)
+        load_x(2, 0, 4)
+        load_w(2)
+        load_w(3)
+        load_x(3, 0, 4)
+        load_biases()
+        load_sw()
+        load_f(0)
+        load_f(1)
+        load_f(2)
+        load_f(3)
+        load_boot()
 
         make_identity(nc, ident[:])
         make_identity(nc, ident_bf[:])
@@ -153,7 +172,10 @@ def tile_reward_continuation_returns_f4_kernel(
             q, head = i // 2, i % 2
             if head == 0:
                 wi[q] = work.tile([P, 2, N, 4], BF16, tag="wi", bufs=2, align_bytes=64, name="wi")
-            nc.scalar.copy(out=wi[q][:, head, :, :], in_=w_raw[i][:].rearrange("p j n -> p n j"))
+            nc.scalar.copy(
+                out=wi[q][:, head, :, :].rearrange("p (c i) j -> p c j i", i=4),
+                in_=w_raw[i][:].rearrange("p j (c i) -> p c j i", i=4),
+            )
 
         def w_quant(q):
             both = slice(2 * q, 2 * q + 2)
@@ -239,9 +261,17 @@ def tile_reward_continuation_returns_f4_kernel(
         def ep_c(k):
             j, g = ORDER[k]
             c2[k] = work.tile([P, 512], F32, tag="c2", bufs=2, name="c2")
-            nc.vector.scalar_tensor_tensor(
-                out=c2[k][:], in0=th[k][:], scalar=1.0, in1=sw_cols[:, 512 * g : 512 * (g + 1)], op0=ALU.add, op1=ALU.mult
-            )
+            weights = sw[:, 512 * g : 512 * (g + 1)].rearrange("p (c h e) -> p h c e", h=2, e=2)
+            for h in range(2):
+                half = slice(256 * h, 256 * (h + 1))
+                nc.vector.scalar_tensor_tensor(
+                    out=c2[k][:, half].rearrange("p (c e) -> p c e", e=2),
+                    in0=th[k][:, half].rearrange("p (c e) -> p c e", e=2),
+                    scalar=1.0,
+                    in1=weights[:, h, :, :],
+                    op0=ALU.add,
+                    op1=ALU.mult,
+                )
 
         def ep_cast(k):
             cy[k] = work.tile([P, 2, 512], BF16, tag="cy", bufs=3, name="cy")
@@ -384,21 +414,23 @@ def tile_reward_continuation_returns_f4_kernel(
             f_turn(i, 0)
             f_turn(i, 1)
 
-        for s in range(4):
-            x_cast(0, s, ("vector", "vector", "vector", "scalar")[s])
-            if s == 1:
-                scale_columns()
-                x_turn(0, 0)
-        x_scale_out(0, 0)
+        x_cast(0, 0, "vector")
+        x_cast(0, 1, "scalar")
+        scale_columns()
+        x_turn(0, 0)
+        x_cast(0, 2, "vector")
+        x_cast(0, 3, "scalar")
         x_turn(0, 1)
+        x_cast(1, 3, "gpsimd")
+        x_cast(1, 0, "scalar")
+        x_cast(1, 2, "gpsimd")
+        x_cast(1, 1, "gpsimd")
+        x_cast(2, 0, "gpsimd")
+        x_cast(2, 1, "gpsimd")
+        x_cast(2, 2, "gpsimd")
+        x_scale_out(0, 0)
+        x_cast(2, 3, "gpsimd")
         x_scale_out(0, 1)
-        for g in range(1, G):
-            for s in range(4):
-                x_cast(g, s, "gpsimd")
-        nc.gpsimd.tensor_copy(
-            out=sw_cols[:].bitcast(F32).rearrange("p (g h c) -> p g h c", g=G, h=2),
-            in_=sw[:].bitcast(F32).rearrange("p (g c h) -> p g h c", g=G, h=2),
-        )
         w_interleave(0)
         w_interleave(1)
         x_turn(1, 0)
@@ -406,22 +438,26 @@ def tile_reward_continuation_returns_f4_kernel(
         x_quant(0)
         x_turn(1, 1)
         x_scale_out(1, 1)
-        w_quant(0)
         w_interleave(2)
-        w_interleave(3)
         bias_columns()
-        w_quant(1)
+        w_interleave(3)
         x_turn(2, 0)
-        turn_f(0)
-        heads(0)
+        x_cast(3, 1, "scalar")
         x_scale_out(2, 0)
+        w_quant(1)
+        turn_f(0)
+        w_quant(0)
         x_turn(2, 1)
+        heads(0)
+        x_cast(3, 0, "scalar")
+        x_scale_out(2, 1)
         x_quant(1)
         act_unit(0)
-        turn_f(1)
-        x_scale_out(2, 1)
-        heads(1)
+        x_cast(3, 2, "scalar")
         x_turn(3, 0)
+        heads(1)
+        x_cast(3, 3, "scalar")
+        turn_f(1)
 
         all_rows = slice(0, S // P)
         both = (0, 1)

@@ -1,3 +1,4 @@
+import math
 from contextlib import ExitStack
 
 import concourse.mybir as mybir
@@ -13,19 +14,24 @@ ACT = mybir.ActivationFunctionType
 ALU = mybir.AluOpType
 
 P = 128
+PACK = 4
+BLOCK = P * PACK
 T, K, N, S = 2048, 1024, 512, 512
-G = T // 512
-KP = K // 512
-J = N // P
-UNITS = J * G
-ORDER = [(j, 2 * half + i) for half in range(2) for j in range(2) for i in range(2)] + [(j, g) for j in (2, 3) for g in range(G)]
-SUMS = {7: (0, 0), 8: (0, 2), 9: (1, 0), 10: (1, 2), 13: (2, 0), 14: (2, 2)}
-FINISH = {8: (0, 0), 9: (0, 1), 10: (1, 0), 11: (1, 1), 14: (2, 0)}
-FLOOR_ON_SCALAR = ()
-LAST_X = (0, 1)
-FILTER_QUANT = (3, 5)
-FILTER_TURN = (1, 2)
-CAST_ON_SCALAR = (1, 2, 3, 4, 5, 6, 8, 14)
+T_BLOCKS = T // BLOCK
+K_PASSES = K // BLOCK
+N_TILES = N // P
+S_TILES = S // P
+
+EARLY_UNITS = [(j, g) for pair in ((0, 1), (2, 3)) for j in (0, 1) for g in pair]
+UNITS = EARLY_UNITS + [(j, g) for j in (2, 3) for g in range(T_BLOCKS)]
+LAST = len(UNITS) - 1
+
+SUMS_AT = {7: (0, 0), 8: (0, 1), 9: (1, 0), 10: (1, 1), 13: (2, 0), 14: (2, 1)}
+FINISH_AT = {k + 1: tile_half for k, tile_half in SUMS_AT.items() if k < LAST - 1}
+MAGNITUDE_AT = {10: 0, 12: 1}
+FILTERS_TURNED_AT = {1: 2, 2: 3}
+FILTERS_QUANTISED_AT = {3: 0, 5: 1}
+ROUND_ON_SCALAR = (0, 1, 2, 3, 5)
 
 FLOPS = 2 * T * K * 2 * N + 2 * S * T * 2 * N
 
@@ -41,511 +47,461 @@ def tile_reward_continuation_returns_f4_kernel(
 
         ident = keep.tile([P, P], F32)
         ident_bf = keep.tile([P, P], BF16)
-        warm = keep.tile([P, 1], F32)
-        b_rows = keep.tile([P, P], BF16)
-        bias = keep.tile([P, 3 * J], F32)
-        scale_raw = keep.tile([P, KP, 4], F32)
-        scale = keep.tile([P, KP, 4, 2], F32)
-        sw = keep.tile([P, T], BF16)
-        boot_sb = keep.tile([P, S // P, N], BF16)
-        xb = [keep.tile([P, 4, K], U8, name="xb%d" % g) for g in range(G)]
-        w_raw = [work.tile([P, 4, N], BF16, tag="raw", bufs=6, name="w_raw") for i in range(2 * KP)]
+        table_dummy = keep.tile([P, 1], F32)
+        bias_rows = keep.tile([P, P], BF16)
+        bias = keep.tile([P, 3 * N_TILES], F32)
+        x_scale_raw = keep.tile([P, K_PASSES, PACK], F32)
+        x_scale_pairs = keep.tile([P, K_PASSES, 4, 2], F32)
+        weights = keep.tile([P, T], BF16)
+        boot_sb = keep.tile([P, S_TILES, N], BF16)
+        x_raw = [keep.tile([P, PACK, K], U8, name="x_raw%d" % g) for g in range(T_BLOCKS)]
+        w_raw = [work.tile([P, PACK, N], BF16, tag="raw", bufs=6, name="w_raw") for i in range(2 * K_PASSES)]
         f_raw = {}
-        f_in = keep.tile([P, G, S, 4], BF16, align_bytes=64)
-        x_codes = keep.tile([P, G * KP, 512], U32, align_bytes=64)
-        x_scales = keep.tile([P, G * KP, 512], U8, align_bytes=64)
-        w_codes = keep.tile([P, 2 * KP, N], U32, align_bytes=64)
-        w_scales = keep.tile([P, 2 * KP, N], U8, align_bytes=64)
-        f_codes = keep.tile([P, G, S], U32, align_bytes=64)
-        f_scales = keep.tile([P, G, S], U8, align_bytes=64)
-        log_sb = keep.tile([P, S // P, N], F32)
-        sign_sb = keep.tile([P, S // P, N], F32)
+        f_grouped = keep.tile([P, T_BLOCKS, S, PACK], BF16, align_bytes=64)
+        x_codes = keep.tile([P, T_BLOCKS * K_PASSES, BLOCK], U32, align_bytes=64)
+        x_scales = keep.tile([P, T_BLOCKS * K_PASSES, BLOCK], U8, align_bytes=64)
+        w_codes = keep.tile([P, 2 * K_PASSES, N], U32, align_bytes=64)
+        w_scales = keep.tile([P, 2 * K_PASSES, N], U8, align_bytes=64)
+        f_codes = keep.tile([P, T_BLOCKS, S], U32, align_bytes=64)
+        f_scales = keep.tile([P, T_BLOCKS, S], U8, align_bytes=64)
+        log_sb = keep.tile([P, S_TILES, N], F32)
+        sign_sb = keep.tile([P, S_TILES, N], F32)
 
         ctx.enter_context(tc.manual_schedule())
 
-        xv = x_bytes.rearrange("(g p s) k -> g p s k", p=P, s=4)
-        wv = [w.rearrange("(q p j) n -> q p j n", p=P, j=4) for w in (w_cont, w_reward)]
-        nc.vector.memset(b_rows[:], 0.0)
-        nc.vector.memset(warm[:], 0.0)
-        nc.scalar.dma_start(out=scale_raw[:], in_=x_scale.rearrange("o (q p t) -> p (o q) t", p=P, t=4))
-        nc.scalar.activation(out=warm[:], in_=warm[:], func=ACT.Exp)
-        def load_x(g, first, last):
-            nc.sync.dma_start(out=xb[g][:, first:last, :], in_=xv[g][:, first:last, :])
+        def head_bank(shape):
+            return psum.tile(shape, F32, tag="heads", bufs=4, name="head_bank")
+
+        def turn_bank(shape, dtype=F32):
+            return psum.tile(shape, dtype, tag="turned", bufs=2, name="turn_bank")
+
+        def sum_bank(shape):
+            return psum.tile(shape, F32, tag="sums", bufs=2, name="sum_bank")
+
+        x_rows = x_bytes.rearrange("(g p s) k -> g p s k", p=P, s=PACK)
+        w_rows = [w.rearrange("(q p j) n -> q p j n", p=P, j=PACK) for w in (w_cont, w_reward)]
+
+        nc.vector.memset(bias_rows[:], 0.0)
+        nc.vector.memset(table_dummy[:], 0.0)
+        nc.scalar.dma_start(out=x_scale_raw[:], in_=x_scale.rearrange("o (q p t) -> p (o q) t", p=P, t=PACK))
+        nc.scalar.activation(out=table_dummy[:], in_=table_dummy[:], func=ACT.Exp)
 
         def load_w(i):
-            nc.sync.dma_start(out=w_raw[i][:], in_=wv[i % 2][i // 2])
+            nc.sync.dma_start(out=w_raw[i][:], in_=w_rows[i % 2][i // 2])
 
-        def load_f(i):
-            f_raw[i] = work.tile([P, T], BF16, tag="raw", bufs=6, name="f_raw")
-            nc.sync.dma_start(out=f_raw[i][:], in_=filters[P * i : P * (i + 1), :])
-
-        def load_biases():
-            nc.sync.dma_start(out=b_rows[0:4, :], in_=b_reward.rearrange("(c p) -> c p", p=P))
-            nc.sync.dma_start(out=b_rows[4:8, :], in_=b_cont.rearrange("(c p) -> c p", p=P))
-
-        def load_sw():
-            nc.sync.dma_start(out=sw[:], in_=step_weight.partition_broadcast(P))
-
-        def load_boot():
-            nc.sync.dma_start(out=boot_sb[:], in_=boot.rearrange("(i p) n -> p i n", p=P))
-
-        load_x(0, 0, 2)
-        load_x(0, 2, 4)
-        load_x(1, 0, 4)
+        nc.sync.dma_start(out=x_raw[0][:, 0:2, :], in_=x_rows[0][:, 0:2, :])
         load_w(0)
+        nc.sync.dma_start(out=x_raw[0][:, 2:4, :], in_=x_rows[0][:, 2:4, :])
+        nc.sync.dma_start(out=x_raw[1][:], in_=x_rows[1])
         load_w(1)
-        load_x(2, 0, 4)
         load_w(2)
         load_w(3)
-        load_x(3, 0, 4)
-        load_biases()
-        load_sw()
-        load_f(0)
-        load_f(1)
-        load_f(2)
-        load_f(3)
-        load_boot()
+        nc.sync.dma_start(out=x_raw[2][:], in_=x_rows[2])
+        nc.sync.dma_start(out=x_raw[3][:], in_=x_rows[3])
+        nc.sync.dma_start(out=bias_rows[0:N_TILES, :], in_=b_reward.rearrange("(c p) -> c p", p=P))
+        nc.sync.dma_start(out=bias_rows[N_TILES : 2 * N_TILES, :], in_=b_cont.rearrange("(c p) -> c p", p=P))
+        nc.sync.dma_start(out=weights[:], in_=step_weight.partition_broadcast(P))
+        for i in range(S_TILES):
+            f_raw[i] = work.tile([P, T], BF16, tag="raw", bufs=6, name="f_raw")
+            nc.sync.dma_start(out=f_raw[i][:], in_=filters[P * i : P * (i + 1), :])
+        nc.sync.dma_start(out=boot_sb[:], in_=boot.rearrange("(i p) n -> p i n", p=P))
 
         make_identity(nc, ident[:])
         make_identity(nc, ident_bf[:])
 
-        def bank(shape, dtype=F32, tag="turned", bufs=2):
-            return psum.tile(shape, dtype, tag=tag, bufs=bufs, name="bank")
+        x_wide, x_turned, x_grouped = {}, {}, {}
 
-        def head_bank(shape):
-            return bank(shape, tag="heads", bufs=4)
-
-        xp = {}
-        xi = {}
-
-        def x_cast(g, s, engine):
-            t = work.tile([P, K], BF16, tag="xp", bufs=6, name="xp")
-            source = xb[g][:, s, :].bitcast(FP8)
+        def widen_x(g, s, engine):
+            x_wide[g, s] = work.tile([P, K], BF16, tag="x_wide", bufs=6, name="x_wide")
+            source = x_raw[g][:, s, :].bitcast(FP8)
             if engine == "scalar":
-                nc.scalar.copy(out=t[:], in_=source)
+                nc.scalar.copy(out=x_wide[g, s][:], in_=source)
             elif engine == "vector":
-                nc.vector.tensor_copy(out=t[:], in_=source)
+                nc.vector.tensor_copy(out=x_wide[g, s][:], in_=source)
             else:
-                nc.gpsimd.tensor_copy(out=t[:], in_=source)
-            xp[g, s] = t
+                nc.gpsimd.tensor_copy(out=x_wide[g, s][:], in_=source)
 
-        def scale_columns():
-            for i in range(2):
+        def pair_scales():
+            for e in range(2):
                 nc.vector.tensor_copy(
-                    out=scale[:, :, 2 * i : 2 * i + 2, :], in_=scale_raw[:].rearrange("p q (u e) -> p q u e", e=2)
+                    out=x_scale_pairs[:, :, 2 * e : 2 * e + 2, :],
+                    in_=x_scale_raw[:].rearrange("p q (u v) -> p q u v", v=2),
                 )
 
-        x_banks = {}
-
-        def x_turn(g, h):
-            for q in range(KP):
-                b = head_bank([P, 4, P]) if g < 2 else bank([P, 4, P], tag="acc")
+        def turn_x(g, h):
+            for q in range(K_PASSES):
+                bank = head_bank([P, 4, P]) if g < 2 else sum_bank([P, 4, P])
                 for e in range(2):
-                    words = xp[g, 2 * h + e][:].bitcast(F32)
+                    words = x_wide[g, 2 * h + e][:].bitcast(F32)
                     for u in range(2):
-                        nc.tensor.transpose(b[:, 2 * e + u, :], words[:, 256 * q + u : 256 * (q + 1) : 2], ident[:])
-                x_banks[g, h, q] = b
+                        nc.tensor.transpose(bank[:, 2 * e + u, :], words[:, 256 * q + u : 256 * (q + 1) : 2], ident[:])
+                x_turned[g, h, q] = bank
 
-        def x_scale_out(g, h):
+        def scale_x(g, h):
             if h == 0:
-                xi[g] = work.tile([P, KP, 512, 4], BF16, tag="xi", bufs=2, align_bytes=64, name="xi")
-            for q in range(KP):
-                part = xi[g][:, q, 2 * P * h : 2 * P * (h + 1), :].rearrange("p c t -> p (c t)")
+                x_grouped[g] = work.tile([P, K_PASSES, BLOCK, PACK], BF16, tag="x_grouped", bufs=2, align_bytes=64, name="x_grouped")
+            for q in range(K_PASSES):
+                half = x_grouped[g][:, q, 256 * h : 256 * (h + 1), :].rearrange("p c t -> p (c t)")
                 nc.vector.tensor_tensor(
-                    out=part.rearrange("p (c w e) -> p c w e", w=4, e=2),
-                    in0=x_banks[g, h, q][:].bitcast(BF16).rearrange("p w (c e) -> p c w e", e=2),
-                    in1=scale[:, q, :, :].unsqueeze(1).to_broadcast([P, P, 4, 2]),
+                    out=half.rearrange("p (c w v) -> p c w v", w=4, v=2),
+                    in0=x_turned[g, h, q][:].bitcast(BF16).rearrange("p w (c v) -> p c w v", v=2),
+                    in1=x_scale_pairs[:, q, :, :].unsqueeze(1).to_broadcast([P, P, 4, 2]),
                     op=ALU.mult,
                 )
 
-        def x_quant(g):
-            both = slice(KP * g, KP * (g + 1))
+        def quantise_x(g):
+            passes = slice(K_PASSES * g, K_PASSES * (g + 1))
             nc.vector.quantize_mx(
-                out=x_codes[:, both, :].rearrange("p q c -> p (q c)").bitcast(FP8X4),
-                scales=x_scales[:, both, :].rearrange("p q c -> p (q c)"),
-                in_=xi[g][:].rearrange("p q c t -> p (q c t)"),
+                out=x_codes[:, passes, :].rearrange("p q c -> p (q c)").bitcast(FP8X4),
+                scales=x_scales[:, passes, :].rearrange("p q c -> p (q c)"),
+                in_=x_grouped[g][:].rearrange("p q c t -> p (q c t)"),
             )
 
-        wi = {}
+        w_grouped = {}
 
-        def w_interleave(i):
+        def group_w(i):
             q, head = i // 2, i % 2
             if head == 0:
-                wi[q] = work.tile([P, 2, N, 4], BF16, tag="wi", bufs=2, align_bytes=64, name="wi")
+                w_grouped[q] = work.tile([P, 2, N, PACK], BF16, tag="w_grouped", bufs=2, align_bytes=64, name="w_grouped")
             nc.scalar.copy(
-                out=wi[q][:, head, :, :].rearrange("p (c i) j -> p c j i", i=4),
+                out=w_grouped[q][:, head, :, :].rearrange("p (c i) j -> p c j i", i=4),
                 in_=w_raw[i][:].rearrange("p j (c i) -> p c j i", i=4),
             )
 
-        def w_quant(q):
-            both = slice(2 * q, 2 * q + 2)
+        def quantise_w(q):
+            heads = slice(2 * q, 2 * q + 2)
             nc.vector.quantize_mx(
-                out=w_codes[:, both, :].rearrange("p i n -> p (i n)").bitcast(FP8X4),
-                scales=w_scales[:, both, :].rearrange("p i n -> p (i n)"),
-                in_=wi[q][:].rearrange("p i n j -> p (i n j)"),
+                out=w_codes[:, heads, :].rearrange("p i n -> p (i n)").bitcast(FP8X4),
+                scales=w_scales[:, heads, :].rearrange("p i n -> p (i n)"),
+                in_=w_grouped[q][:].rearrange("p i n j -> p (i n j)"),
             )
 
-        f_words = f_in[:].rearrange("p g s t -> p (g s t)").bitcast(F32).rearrange("p (g s u) -> p g s u", g=G, u=2)
+        def bias_columns():
+            turned = turn_bank([P, P], BF16)
+            nc.tensor.transpose(turned[:], bias_rows[:], ident_bf[:])
+            for group, source, factor, added in ((0, 0, 1.0, 0.0), (1, 1, -0.5, 0.0), (2, 0, -1.0, -math.log(2.0))):
+                nc.vector.tensor_scalar(
+                    out=bias[:, N_TILES * group : N_TILES * (group + 1)],
+                    in0=turned[:, N_TILES * source : N_TILES * (source + 1)],
+                    scalar1=factor,
+                    scalar2=added,
+                    op0=ALU.mult,
+                    op1=ALU.add,
+                )
 
-        def f_turn(i, h):
+        f_words = f_grouped[:].rearrange("p g s t -> p (g s t)").bitcast(F32)
+        f_words = f_words.rearrange("p (g s u) -> p g s u", g=T_BLOCKS, u=2)
+
+        def turn_filters(i):
             words = f_raw[i][:].bitcast(F32)
-            b = bank([P, 4, P])
-            for g in range(2):
-                for u in range(2):
+            for h in range(2):
+                bank = turn_bank([P, 4, P])
+                for g in range(2):
                     first = 256 * (2 * h + g)
-                    nc.tensor.transpose(b[:, 2 * g + u, :], words[:, first + u : first + 256 : 2], ident[:])
-            nc.scalar.copy(
-                out=f_words[:, 2 * h : 2 * h + 2, P * i : P * (i + 1), :],
-                in_=b[:].rearrange("p (g u) s -> p g s u", u=2),
-            )
+                    for u in range(2):
+                        nc.tensor.transpose(bank[:, 2 * g + u, :], words[:, first + u : first + 256 : 2], ident[:])
+                nc.scalar.copy(
+                    out=f_words[:, 2 * h : 2 * h + 2, P * i : P * (i + 1), :],
+                    in_=bank[:].rearrange("p (g u) s -> p g s u", u=2),
+                )
 
-        def f_quant(h):
-            two = slice(2 * h, 2 * h + 2)
+        def quantise_filters(h):
+            blocks = slice(2 * h, 2 * h + 2)
             nc.vector.quantize_mx(
-                out=f_codes[:, two, :].rearrange("p g s -> p (g s)").bitcast(FP8X4),
-                scales=f_scales[:, two, :].rearrange("p g s -> p (g s)"),
-                in_=f_in[:, two, :, :].rearrange("p g s t -> p (g s t)"),
+                out=f_codes[:, blocks, :].rearrange("p g s -> p (g s)").bitcast(FP8X4),
+                scales=f_scales[:, blocks, :].rearrange("p g s -> p (g s)"),
+                in_=f_grouped[:, blocks, :, :].rearrange("p g s t -> p (g s t)"),
             )
 
-        zc, zr, th, e1, e2, cy, tb, cyi = {}, {}, {}, {}, {}, {}, {}, {}
+        zc, zr, tanh_neg, exp_pos, exp_neg, c_minus2, cy, cy_turned, cy_grouped = {}, {}, {}, {}, {}, {}, {}, {}, {}
         cy_codes, cy_scales = {}, {}
 
-        def heads(k):
-            j, g = ORDER[k]
+        def multiply_heads(k):
+            j, g = UNITS[k]
             cols = slice(P * j, P * (j + 1))
             for head, store in ((0, zc), (1, zr)):
-                b = head_bank([P, 512])
-                for q in range(KP):
+                store[k] = head_bank([P, BLOCK])
+                for q in range(K_PASSES):
                     nc.tensor.matmul_mx(
-                        out=b[:],
+                        out=store[k][:],
                         lhsT=w_codes[:, 2 * q + head, cols].bitcast(FP8X4),
                         lhsT_scale=w_scales[:, 2 * q + head, cols],
-                        rhs=x_codes[:, KP * g + q, :].bitcast(FP8X4),
-                        rhs_scale=x_scales[:, KP * g + q, :],
+                        rhs=x_codes[:, K_PASSES * g + q, :].bitcast(FP8X4),
+                        rhs_scale=x_scales[:, K_PASSES * g + q, :],
                         start=(q == 0),
-                        stop=(q == KP - 1),
+                        stop=(q == K_PASSES - 1),
                     )
-                store[k] = b
 
-        def act_tanh(k):
-            j, g = ORDER[k]
-            t = work.tile([P, 512], F32, tag="th", bufs=3, name="th")
-            nc.scalar.activation(out=t[:], in_=zc[k][:], func=ACT.Tanh, bias=bias[:, J + j : J + j + 1], scale=0.5)
-            th[k] = t
+        def activate(out, source, k, func, group, factor):
+            column = N_TILES * group + UNITS[k][0]
+            nc.scalar.activation(out=out[:], in_=source[:], func=func, bias=bias[:, column : column + 1], scale=factor)
 
-        def act_unit_start(k):
-            j, g = ORDER[k]
-            e2[k] = work.tile([P, 512], F32, tag="e2", bufs=3, name="e2")
-            if k in FLOOR_ON_SCALAR:
-                nc.scalar.activation(
-                    out=e2[k][:], in_=zr[k][:], func=ACT.Relu, bias=bias[:, 2 * J + j : 2 * J + j + 1], scale=-1.0
-                )
-            act_tanh(k)
-            act_exp_minus(k)
+        def take_tanh(k):
+            tanh_neg[k] = work.tile([P, BLOCK], F32, tag="tanh_neg", bufs=3, name="tanh_neg")
+            activate(tanh_neg[k], zc[k], k, ACT.Tanh, 1, -0.5)
 
-        def act_exp_minus(k):
-            j, g = ORDER[k]
-            source, offset, factor = zr[k], bias[:, 2 * J + j : 2 * J + j + 1], -1.0
-            if k in FLOOR_ON_SCALAR:
-                source, offset, factor = e2[k], 0.0, 1.0
-            nc.scalar.activation(out=e2[k][:], in_=source[:], func=ACT.Exp, bias=offset, scale=factor)
+        def take_exp_pos(k):
+            exp_pos[k] = work.tile([P, BLOCK], F32, tag="exp_pos", bufs=3, name="exp_pos")
+            activate(exp_pos[k], zr[k], k, ACT.Exp, 0, 1.0)
 
-        def act_exp_plus(k):
-            j, g = ORDER[k]
-            t = work.tile([P, 512], F32, tag="e1", bufs=3, name="e1")
-            nc.scalar.activation(out=t[:], in_=zr[k][:], func=ACT.Exp, bias=bias[:, j : j + 1], scale=1.0)
-            e1[k] = t
+        def take_exp_neg(k):
+            exp_neg[k] = work.tile([P, BLOCK], F32, tag="exp_neg", bufs=3, name="exp_neg")
+            activate(exp_neg[k], zr[k], k, ACT.Exp, 2, -1.0)
 
-        c2 = {}
-
-        def ep_c(k):
-            j, g = ORDER[k]
-            c2[k] = work.tile([P, 512], F32, tag="c2", bufs=2, name="c2")
-            weights = sw[:, 512 * g : 512 * (g + 1)].rearrange("p (c h e) -> p h c e", h=2, e=2)
+        def weigh(k):
+            g = UNITS[k][1]
+            c_minus2[k] = work.tile([P, BLOCK], F32, tag="c_minus2", bufs=2, name="c_minus2")
+            w_cols = weights[:, BLOCK * g : BLOCK * (g + 1)].rearrange("p (c h e) -> p h c e", h=2, e=2)
             for h in range(2):
                 half = slice(256 * h, 256 * (h + 1))
                 nc.vector.scalar_tensor_tensor(
-                    out=c2[k][:, half].rearrange("p (c e) -> p c e", e=2),
-                    in0=th[k][:, half].rearrange("p (c e) -> p c e", e=2),
+                    out=c_minus2[k][:, half].rearrange("p (c e) -> p c e", e=2),
+                    in0=tanh_neg[k][:, half].rearrange("p (c e) -> p c e", e=2),
                     scalar=1.0,
-                    in1=weights[:, h, :, :],
-                    op0=ALU.add,
+                    in1=w_cols[:, h, :, :],
+                    op0=ALU.subtract,
                     op1=ALU.mult,
                 )
 
-        def ep_cast(k):
-            cy[k] = work.tile([P, 2, 512], BF16, tag="cy", bufs=3, name="cy")
-            if k in CAST_ON_SCALAR:
-                nc.scalar.activation(out=cy[k][:, 0, :], in_=c2[k][:], func=ACT.Copy, scale=0.5)
+        def round_c(k):
+            cy[k] = work.tile([P, 2, BLOCK], BF16, tag="cy", bufs=3, name="cy")
+            if k in ROUND_ON_SCALAR:
+                nc.scalar.activation(out=cy[k][:, 0, :], in_=c_minus2[k][:], func=ACT.Copy, scale=-0.5)
             else:
-                nc.vector.tensor_scalar(out=cy[k][:, 0, :], in0=c2[k][:], scalar1=0.5, scalar2=None, op0=ALU.mult)
+                nc.vector.tensor_scalar(out=cy[k][:, 0, :], in0=c_minus2[k][:], scalar1=-0.5, scalar2=None, op0=ALU.mult)
 
-        def ep_floor(k):
-            if k not in FLOOR_ON_SCALAR:
-                nc.vector.tensor_scalar(out=e2[k][:], in0=e2[k][:], scalar1=1.0, scalar2=None, op0=ALU.max)
-
-        def ep_symexp(k):
+        def multiply_c(k):
             nc.vector.scalar_tensor_tensor(
-                out=e1[k][:], in0=e1[k][:], scalar=1.0, in1=e2[k][:], op0=ALU.max, op1=ALU.subtract
+                out=exp_pos[k][:], in0=exp_pos[k][:], scalar=1.0, in1=c_minus2[k][:], op0=ALU.max, op1=ALU.mult
             )
 
-        def ep_y(k):
+        def make_y(k):
             nc.vector.scalar_tensor_tensor(
-                out=cy[k][:, 1, :], in0=c2[k][:], scalar=0.5, in1=e1[k][:], op0=ALU.mult, op1=ALU.mult
+                out=cy[k][:, 1, :], in0=exp_neg[k][:], scalar=0.5, in1=exp_pos[k][:], op0=ALU.subtract, op1=ALU.mult
             )
 
-        def turn(k, kinds):
-            b = bank([P, len(kinds), 2, P])
+        def turn_cy(k, kinds):
+            cy_turned[k, kinds[0]] = turn_bank([P, len(kinds), 2, P])
             for n, kind in enumerate(kinds):
                 words = cy[k][:, kind, :].bitcast(F32)
                 for h in range(2):
-                    nc.tensor.transpose(b[:, n, h, :], words[:, P * h : P * (h + 1)], ident[:])
-            tb[k, kinds[0]] = b
+                    nc.tensor.transpose(cy_turned[k, kinds[0]][:, n, h, :], words[:, P * h : P * (h + 1)], ident[:])
 
-        def turn_out(k, kinds):
+        def group_cy(k, kinds):
             if kinds[0] == 0:
-                cyi[k] = work.tile([P, 2, P, 4], BF16, tag="cyi", bufs=3, align_bytes=64, name="cyi")
-            part = cyi[k][:, kinds[0] : kinds[0] + len(kinds), :, :]
+                cy_grouped[k] = work.tile([P, 2, P, PACK], BF16, tag="cy_grouped", bufs=3, align_bytes=64, name="cy_grouped")
+            part = cy_grouped[k][:, kinds[0] : kinds[0] + len(kinds), :, :]
             nc.scalar.copy(
                 out=part.rearrange("p w n t -> p (w n t)").bitcast(F32).rearrange("p (w n h) -> p w n h", n=P, h=2),
-                in_=tb[k, kinds[0]][:].rearrange("p w h n -> p w n h"),
+                in_=cy_turned[k, kinds[0]][:].rearrange("p w h n -> p w n h"),
             )
 
-        def turn_quant(k, kinds):
-            j, g = ORDER[k]
+        def quantise_cy(k, kinds):
+            j, g = UNITS[k]
             if g == 0:
-                cy_codes[j] = work.tile([P, G, 2 * P], U32, tag="cy_codes", bufs=3, align_bytes=64, name="cy_codes")
-                cy_scales[j] = work.tile([P, G, 2 * P], U8, tag="cy_scales", bufs=3, align_bytes=64, name="cy_scales")
+                cy_codes[j] = work.tile([P, T_BLOCKS, 2 * P], U32, tag="cy_codes", bufs=3, align_bytes=64, name="cy_codes")
+                cy_scales[j] = work.tile([P, T_BLOCKS, 2 * P], U8, tag="cy_scales", bufs=3, align_bytes=64, name="cy_scales")
             cols = slice(P * kinds[0], P * (kinds[0] + len(kinds)))
             nc.vector.quantize_mx(
                 out=cy_codes[j][:, g, cols].bitcast(FP8X4),
                 scales=cy_scales[j][:, g, cols],
-                in_=cyi[k][:, kinds[0] : kinds[0] + len(kinds), :, :].rearrange("p w n t -> p (w n t)"),
+                in_=cy_grouped[k][:, kinds[0] : kinds[0] + len(kinds), :, :].rearrange("p w n t -> p (w n t)"),
             )
 
-        acc = {}
+        mass_rows = out_1.rearrange("(i p) n -> p i n", p=P)
+        ret_rows = out_0.rearrange("(i p) n -> p i n", p=P)
+        sums, boot_terms, returns = {}, {}, {}
 
-        def filter_pass(j, i, g, out, cols):
+        def task_cols(j):
+            return slice(P * j, P * (j + 1))
+
+        def sum_pass(j, i, g, out):
             nc.tensor.matmul_mx(
                 out=out,
                 lhsT=f_codes[:, g, P * i : P * (i + 1)].bitcast(FP8X4),
                 lhsT_scale=f_scales[:, g, P * i : P * (i + 1)],
-                rhs=cy_codes[j][:, g, cols].bitcast(FP8X4),
-                rhs_scale=cy_scales[j][:, g, cols],
+                rhs=cy_codes[j][:, g, :].bitcast(FP8X4),
+                rhs_scale=cy_scales[j][:, g, :],
                 start=(g == 0),
-                stop=(g == G - 1),
+                stop=(g == T_BLOCKS - 1),
             )
 
-        def filter_sums(j, i):
-            if i % 2 == 0:
-                acc[j, i // 2] = bank([P, 2, 2 * P], tag="acc")
-            for g in range(G):
-                filter_pass(j, i, g, acc[j, i // 2][:, i % 2, :], slice(0, 2 * P))
+        def sum_half(j, h):
+            sums[j, h] = sum_bank([P, 2, 2 * P])
+            for i in range(2):
+                for g in range(T_BLOCKS):
+                    sum_pass(j, 2 * h + i, g, sums[j, h][:, i, :])
 
-        mass_out = out_1.rearrange("(i p) n -> p i n", p=P)
-        ret_out = out_0.rearrange("(i p) n -> p i n", p=P)
-        t2 = {}
+        def bootstrap(j, h):
+            rows, cols = slice(2 * h, 2 * h + 2), task_cols(j)
+            mass = work.tile([P, 2, P], F32, tag="mass", bufs=2, name="mass")
+            nc.scalar.copy(out=mass[:], in_=sums[j, h][:, :, 0:P])
+            nc.sync.dma_start(out=mass_rows[:, rows, cols], in_=mass[:])
+            boot_terms[j, h] = work.tile([P, 2, P], F32, tag="boot_term", bufs=2, name="boot_term")
+            nc.vector.tensor_tensor(
+                out=boot_terms[j, h][:], in0=sums[j, h][:, :, 0:P], in1=boot_sb[:, rows, cols], op=ALU.mult
+            )
 
-        t1s = {}
-
-        def finish_product(j, h):
-            rows, cols = slice(2 * h, 2 * h + 2), slice(P * j, P * (j + 1))
-            a = acc[j, h][:]
-            ms = work.tile([P, 2, P], F32, tag="ms", bufs=2, name="ms")
-            nc.scalar.copy(out=ms[:], in_=a[:, :, 0:P])
-            nc.sync.dma_start(out=mass_out[:, rows, cols], in_=ms[:])
-            t1 = work.tile([P, 2, P], F32, tag="t1", bufs=2, name="t1")
-            nc.vector.tensor_tensor(out=t1[:], in0=a[:, :, 0:P], in1=boot_sb[:, rows, cols], op=ALU.mult)
-            t1s[j, h] = t1
-
-        def finish_add(j, h):
-            rows, cols = slice(2 * h, 2 * h + 2), slice(P * j, P * (j + 1))
-            a = acc[j, h][:]
-            t1 = t1s[j, h]
+        def add_gain(j, h):
             if h == 0:
-                t2[j] = work.tile([P, 4, P], F32, tag="t2", bufs=2, name="t2")
-            nc.vector.tensor_tensor(out=t2[j][:, rows, :], in0=a[:, :, P : 2 * P], in1=t1[:], op=ALU.add)
+                returns[j] = work.tile([P, S_TILES, P], F32, tag="returns", bufs=2, name="returns")
+            nc.vector.tensor_tensor(
+                out=returns[j][:, 2 * h : 2 * h + 2, :], in0=sums[j, h][:, :, P : 2 * P], in1=boot_terms[j, h][:], op=ALU.add
+            )
 
-        def finish_abs(j):
-            cols = slice(P * j, P * (j + 1))
-            nc.scalar.activation(out=log_sb[:, :, cols], in_=t2[j][:], func=ACT.Abs)
+        def magnitude(j):
+            nc.scalar.activation(out=log_sb[:, :, task_cols(j)], in_=returns[j][:], func=ACT.Abs)
 
-        def finish_sign(j):
-            cols = slice(P * j, P * (j + 1))
-            if j < 2:
-                nc.scalar.activation(out=sign_sb[:, :, cols], in_=t2[j][:], func=ACT.Sign)
-            else:
-                nc.vector.tensor_scalar(
-                    out=sign_sb[:, :, cols], in0=t2[j][:], scalar1=0.0, scalar2=2.0, op0=ALU.is_ge, op1=ALU.mult
-                )
+        def sign_on_scalar(j):
+            nc.scalar.activation(out=sign_sb[:, :, task_cols(j)], in_=returns[j][:], func=ACT.Sign)
 
-        def symlog(rows, cols):
-            nc.scalar.activation(out=log_sb[:, rows, cols], in_=log_sb[:, rows, cols], func=ACT.Ln, bias=1.0, scale=1.0)
+        def half_sign_on_vector(j):
+            nc.vector.tensor_scalar(
+                out=sign_sb[:, :, task_cols(j)], in0=returns[j][:], scalar1=0.0, scalar2=0.5, op0=ALU.is_ge, op1=ALU.subtract
+            )
 
-        def symlog_store(j, cols):
-            if j < 2:
-                nc.vector.tensor_tensor(
-                    out=log_sb[:, :, cols], in0=log_sb[:, :, cols], in1=sign_sb[:, :, cols], op=ALU.mult
-                )
-            else:
-                nc.vector.scalar_tensor_tensor(
-                    out=log_sb[:, :, cols],
-                    in0=sign_sb[:, :, cols],
-                    scalar=-1.0,
-                    in1=log_sb[:, :, cols],
-                    op0=ALU.add,
-                    op1=ALU.mult,
-                )
-            nc.sync.dma_start(out=ret_out[:, :, cols], in_=log_sb[:, :, cols])
+        def take_log(cols):
+            nc.scalar.activation(out=log_sb[:, :, cols], in_=log_sb[:, :, cols], func=ACT.Ln, bias=1.0, scale=1.0)
 
-        def bias_columns():
-            b_t = bank([P, P], BF16)
-            nc.tensor.transpose(b_t[:], b_rows[:], ident_bf[:])
-            for first, source, factor in ((0, 0, 1.0), (J, J, 0.5), (2 * J, 0, -1.0)):
-                nc.vector.tensor_scalar(
-                    out=bias[:, first : first + J], in0=b_t[:, source : source + J], scalar1=factor, scalar2=None, op0=ALU.mult
-                )
+        def store_returns(cols, factor):
+            nc.vector.scalar_tensor_tensor(
+                out=log_sb[:, :, cols],
+                in0=sign_sb[:, :, cols],
+                scalar=factor,
+                in1=log_sb[:, :, cols],
+                op0=ALU.mult,
+                op1=ALU.mult,
+            )
+            nc.sync.dma_start(out=ret_rows[:, :, cols], in_=log_sb[:, :, cols])
 
-        def act_unit(k):
-            act_unit_start(k)
-            act_exp_plus(k)
-
-        def turn_f(i):
-            f_turn(i, 0)
-            f_turn(i, 1)
-
-        x_cast(0, 0, "vector")
-        x_cast(0, 1, "scalar")
-        scale_columns()
-        x_turn(0, 0)
-        x_cast(0, 2, "vector")
-        x_cast(0, 3, "scalar")
-        x_turn(0, 1)
-        x_cast(1, 3, "gpsimd")
-        x_cast(1, 0, "scalar")
-        x_cast(1, 2, "gpsimd")
-        x_cast(1, 1, "gpsimd")
-        x_cast(2, 0, "gpsimd")
-        x_cast(2, 1, "gpsimd")
-        x_cast(2, 2, "gpsimd")
-        x_scale_out(0, 0)
-        x_cast(2, 3, "gpsimd")
-        x_scale_out(0, 1)
-        w_interleave(0)
-        w_interleave(1)
-        x_turn(1, 0)
-        x_scale_out(1, 0)
-        x_quant(0)
-        x_turn(1, 1)
-        x_scale_out(1, 1)
-        w_interleave(2)
+        for s in range(4):
+            widen_x(0, s, "vector" if s % 2 == 0 else "scalar")
+            if s == 0:
+                pair_scales()
+            if s % 2 == 1:
+                turn_x(0, s // 2)
+        widen_x(1, 0, "scalar")
+        for g, s in [(1, 1), (1, 2), (1, 3), (2, 0), (2, 1), (2, 2), (2, 3)]:
+            widen_x(g, s, "gpsimd")
+        for h in range(2):
+            scale_x(0, h)
+            group_w(h)
+        for h in range(2):
+            turn_x(1, h)
+            scale_x(1, h)
+        quantise_x(0)
+        group_w(2)
         bias_columns()
-        w_interleave(3)
-        x_turn(2, 0)
-        x_cast(3, 1, "scalar")
-        x_scale_out(2, 0)
-        w_quant(1)
-        turn_f(0)
-        w_quant(0)
-        x_turn(2, 1)
-        heads(0)
-        x_cast(3, 0, "scalar")
-        x_scale_out(2, 1)
-        x_quant(1)
-        act_unit(0)
-        x_cast(3, 2, "scalar")
-        x_turn(3, 0)
-        heads(1)
-        x_cast(3, 3, "scalar")
-        turn_f(1)
+        group_w(3)
+        turn_x(2, 0)
+        widen_x(3, 0, "scalar")
+        scale_x(2, 0)
+        turn_filters(0)
+        quantise_w(0)
+        quantise_w(1)
+        turn_x(2, 1)
+        widen_x(3, 1, "scalar")
+        scale_x(2, 1)
+        quantise_x(1)
+        multiply_heads(0)
+        widen_x(3, 2, "scalar")
+        take_tanh(0)
+        take_exp_pos(0)
+        take_exp_neg(0)
+        widen_x(3, 3, "scalar")
+        turn_filters(1)
+        turn_x(3, 0)
+        multiply_heads(1)
+        weigh(0)
 
-        all_rows = slice(0, S // P)
-        both = (0, 1)
-        tail = {}
-        last = UNITS - 1
-        for k in range(last):
+        both = range(2)
+        for k in range(LAST):
             if k >= 1:
-                turn(k - 1, both)
-            if k + 2 < UNITS:
-                heads(k + 2)
-            act_unit_start(k + 1)
-            ep_floor(k)
-            ep_c(k)
-            ep_symexp(k)
-            if k in FINISH:
-                finish_product(*FINISH[k])
+                turn_cy(k - 1, both)
+            if k + 2 <= LAST:
+                multiply_heads(k + 2)
+            take_tanh(k + 1)
+            take_exp_pos(k + 1)
+            multiply_c(k)
+            round_c(k)
+            if k in FINISH_AT:
+                bootstrap(*FINISH_AT[k])
             if k >= 1:
-                turn_out(k - 1, both)
-            ep_cast(k)
-            act_exp_plus(k + 1)
-            if k in LAST_X:
-                x_scale_out(3, LAST_X.index(k))
-            if k in FILTER_QUANT:
-                f_quant(FILTER_QUANT.index(k))
+                group_cy(k - 1, both)
+            take_exp_neg(k + 1)
+            if k <= 1:
+                scale_x(3, k)
+            if k in FILTERS_QUANTISED_AT:
+                quantise_filters(FILTERS_QUANTISED_AT[k])
+            make_y(k)
+            weigh(k + 1)
             if k >= 1:
-                turn_quant(k - 1, both)
-            ep_y(k)
-            if k == LAST_X[1] - 1:
-                x_turn(3, 1)
-            if k in FILTER_TURN:
-                turn_f(2 + FILTER_TURN.index(k))
+                quantise_cy(k - 1, both)
             if k == 0:
-                x_quant(2)
+                turn_x(3, 1)
+            if k in FILTERS_TURNED_AT:
+                turn_filters(FILTERS_TURNED_AT[k])
+            if k == 0:
+                quantise_x(2)
             if k == 2:
-                x_quant(3)
-            if k in FINISH:
-                finish_add(*FINISH[k])
-            if k in SUMS:
-                j, i = SUMS[k]
-                filter_sums(j, i)
-                filter_sums(j, i + 1)
-            if k in (10, 12):
-                finish_abs((k - 10) // 2)
-                finish_sign((k - 10) // 2)
-        turn(last - 1, both)
-        turn_out(last - 1, both)
-        ep_c(last)
-        ep_floor(last)
-        ep_cast(last)
-        turn(last, (0,))
-        turn_out(last, (0,))
-        finish_product(2, 1)
-        ep_symexp(last)
-        turn_quant(last - 1, both)
-        finish_add(2, 1)
-        for i in range(S // P):
-            tail[i] = head_bank([P, P])
-        for g in range(3):
-            for i in range(S // P):
-                filter_pass(3, i, g, tail[i][:], slice(P, 2 * P))
-        turn_quant(last, (0,))
-        ep_y(last)
-        nc.scalar.activation(out=warm[:], in_=warm[:], func=ACT.Ln, bias=1.0)
-        mass = bank([P, 4, P])
-        for i in range(S // P):
-            if i == 2:
-                turn(last, (1,))
-            for g in range(G):
-                filter_pass(3, i, g, mass[:, i, :], slice(0, P))
-        turn_out(last, (1,))
-        cols = slice(3 * P, 4 * P)
-        t1 = work.tile([P, 4, P], F32, tag="t1", bufs=2, name="t1")
-        ms = work.tile([P, 4, P], F32, tag="ms", bufs=2, name="ms")
-        t2[3] = work.tile([P, 4, P], F32, tag="t2", bufs=2, name="t2")
-        finish_sign(2)
-        turn_quant(last, (1,))
-        nc.vector.tensor_tensor(out=t1[:], in0=mass[:], in1=boot_sb[:, :, cols], op=ALU.mult)
-        finish_abs(2)
-        symlog(all_rows, slice(0, 3 * P))
-        for i in range(S // P):
-            filter_pass(3, i, 3, tail[i][:], slice(P, 2 * P))
-        nc.vector.tensor_copy(out=ms[:], in_=mass[:])
-        nc.sync.dma_start(out=mass_out[:, :, cols], in_=ms[:])
-        for i in range(S // P):
-            nc.vector.tensor_tensor(out=t2[3][:, i, :], in0=tail[i][:], in1=t1[:, i, :], op=ALU.add)
-        finish_abs(3)
-        symlog(all_rows, cols)
-        finish_sign(3)
-        symlog_store(0, slice(0, 2 * P))
-        symlog_store(2, slice(2 * P, 3 * P))
-        symlog_store(3, cols)
+                quantise_x(3)
+            if k in FINISH_AT:
+                add_gain(*FINISH_AT[k])
+            if k in SUMS_AT:
+                sum_half(*SUMS_AT[k])
+            if k in MAGNITUDE_AT:
+                magnitude(MAGNITUDE_AT[k])
+                sign_on_scalar(MAGNITUDE_AT[k])
+
+        early, late = slice(0, 2 * P), slice(2 * P, 3 * P)
+        tail_cols = task_cols(3)
+        tail = [head_bank([P, 2 * P]) for i in range(S_TILES)]
+
+        def tail_passes(g):
+            for i in range(S_TILES):
+                sum_pass(3, i, g, tail[i][:])
+
+        turn_cy(LAST - 1, both)
+        group_cy(LAST - 1, both)
+        take_log(early)
+        round_c(LAST)
+        multiply_c(LAST)
+        tail_passes(0)
+        tail_passes(1)
+        turn_cy(LAST, range(0, 1))
+        group_cy(LAST, range(0, 1))
+        bootstrap(2, 1)
+        quantise_cy(LAST - 1, both)
+        add_gain(2, 1)
+        tail_passes(2)
+        make_y(LAST)
+        turn_cy(LAST, range(1, 2))
+        group_cy(LAST, range(1, 2))
+        half_sign_on_vector(2)
+        quantise_cy(LAST, range(0, 1))
+        quantise_cy(LAST, range(1, 2))
+        magnitude(2)
+        take_log(late)
+        tail_passes(3)
+
+        tail_mass = work.tile([P, S_TILES, P], F32, tag="mass", bufs=2, name="tail_mass")
+        tail_boot = work.tile([P, S_TILES, P], F32, tag="boot_term", bufs=2, name="tail_boot")
+        returns[3] = work.tile([P, S_TILES, P], F32, tag="returns", bufs=2, name="returns")
+        store_returns(early, 1.0)
+        for i in range(S_TILES + 1):
+            if i < S_TILES:
+                nc.vector.tensor_tensor(
+                    out=tail_boot[:, i, :], in0=tail[i][:, 0:P], in1=boot_sb[:, i, tail_cols], op=ALU.mult
+                )
+            if i >= 1:
+                nc.vector.tensor_tensor(
+                    out=returns[3][:, i - 1, :], in0=tail[i - 1][:, P : 2 * P], in1=tail_boot[:, i - 1, :], op=ALU.add
+                )
+        for i in range(S_TILES):
+            nc.scalar.copy(out=tail_mass[:, i, :], in_=tail[i][:, 0:P])
+        nc.sync.dma_start(out=mass_rows[:, :, tail_cols], in_=tail_mass[:])
+        magnitude(3)
+        take_log(tail_cols)
+        store_returns(late, 2.0)
+        half_sign_on_vector(3)
+        store_returns(tail_cols, 2.0)

import math
from contextlib import ExitStack

import concourse.mybir as mybir
from concourse.masks import make_identity

F32 = mybir.dt.float32
BF16 = mybir.dt.bfloat16
U32 = mybir.dt.uint32
U8 = mybir.dt.uint8
FP8 = mybir.dt.float8_e4m3fn
FP8X4 = mybir.dt.float8_e4m3fn_x4
ACT = mybir.ActivationFunctionType
ALU = mybir.AluOpType

P = 128
PACK = 4
BLOCK = P * PACK
T, K, N, S = 2048, 1024, 512, 512
T_BLOCKS = T // BLOCK
K_PASSES = K // BLOCK
N_TILES = N // P
S_TILES = S // P

EARLY_UNITS = [(j, g) for pair in ((0, 1), (2, 3)) for j in (0, 1) for g in pair]
UNITS = EARLY_UNITS + [(j, g) for j in (2, 3) for g in range(T_BLOCKS)]
LAST = len(UNITS) - 1

SUMS_AT = {7: (0, 0), 8: (0, 1), 9: (1, 0), 10: (1, 1), 13: (2, 0), 14: (2, 1)}
FINISH_AT = {k + 1: tile_half for k, tile_half in SUMS_AT.items() if k < LAST - 1}
MAGNITUDE_AT = {10: 0, 12: 1}
FILTERS_TURNED_AT = {1: 2, 2: 3}
FILTERS_QUANTISED_AT = {3: 0, 5: 1}
ROUND_ON_SCALAR = (0, 1, 2, 3, 5)

FLOPS = 2 * T * K * 2 * N + 2 * S * T * 2 * N


def tile_reward_continuation_returns_f4_kernel(
    tc, x_bytes, x_scale, w_reward, w_cont, b_reward, b_cont, step_weight, filters, boot, out_0, out_1
):
    nc = tc.nc
    with ExitStack() as ctx:
        keep = ctx.enter_context(tc.tile_pool(name="keep", bufs=1))
        work = ctx.enter_context(tc.tile_pool(name="work", bufs=2))
        psum = ctx.enter_context(tc.psum_pool(name="psum", bufs=1))

        ident = keep.tile([P, P], F32)
        ident_bf = keep.tile([P, P], BF16)
        table_dummy = keep.tile([P, 1], F32)
        bias_rows = keep.tile([P, P], BF16)
        bias = keep.tile([P, 3 * N_TILES], F32)
        x_scale_raw = keep.tile([P, K_PASSES, PACK], F32)
        x_scale_pairs = keep.tile([P, K_PASSES, 4, 2], F32)
        weights = keep.tile([P, T], BF16)
        boot_sb = keep.tile([P, S_TILES, N], BF16)
        x_raw = [keep.tile([P, PACK, K], U8, name="x_raw%d" % g) for g in range(T_BLOCKS)]
        w_raw = [work.tile([P, PACK, N], BF16, tag="raw", bufs=6, name="w_raw") for i in range(2 * K_PASSES)]
        f_raw = {}
        f_grouped = keep.tile([P, T_BLOCKS, S, PACK], BF16, align_bytes=64)
        x_codes = keep.tile([P, T_BLOCKS * K_PASSES, BLOCK], U32, align_bytes=64)
        x_scales = keep.tile([P, T_BLOCKS * K_PASSES, BLOCK], U8, align_bytes=64)
        w_codes = keep.tile([P, 2 * K_PASSES, N], U32, align_bytes=64)
        w_scales = keep.tile([P, 2 * K_PASSES, N], U8, align_bytes=64)
        f_codes = keep.tile([P, T_BLOCKS, S], U32, align_bytes=64)
        f_scales = keep.tile([P, T_BLOCKS, S], U8, align_bytes=64)
        log_sb = keep.tile([P, S_TILES, N], F32)
        sign_sb = keep.tile([P, S_TILES, N], F32)

        ctx.enter_context(tc.manual_schedule())

        def head_bank(shape):
            return psum.tile(shape, F32, tag="heads", bufs=4, name="head_bank")

        def turn_bank(shape, dtype=F32):
            return psum.tile(shape, dtype, tag="turned", bufs=2, name="turn_bank")

        def sum_bank(shape):
            return psum.tile(shape, F32, tag="sums", bufs=2, name="sum_bank")

        x_rows = x_bytes.rearrange("(g p s) k -> g p s k", p=P, s=PACK)
        w_rows = [w.rearrange("(q p j) n -> q p j n", p=P, j=PACK) for w in (w_cont, w_reward)]

        nc.vector.memset(bias_rows[:], 0.0)
        nc.vector.memset(table_dummy[:], 0.0)
        nc.scalar.dma_start(out=x_scale_raw[:], in_=x_scale.rearrange("o (q p t) -> p (o q) t", p=P, t=PACK))
        nc.scalar.activation(out=table_dummy[:], in_=table_dummy[:], func=ACT.Exp)

        def load_w(i):
            nc.sync.dma_start(out=w_raw[i][:], in_=w_rows[i % 2][i // 2])

        nc.sync.dma_start(out=x_raw[0][:, 0:2, :], in_=x_rows[0][:, 0:2, :])
        load_w(0)
        nc.sync.dma_start(out=x_raw[0][:, 2:4, :], in_=x_rows[0][:, 2:4, :])
        nc.sync.dma_start(out=x_raw[1][:], in_=x_rows[1])
        load_w(1)
        load_w(2)
        load_w(3)
        nc.sync.dma_start(out=x_raw[2][:], in_=x_rows[2])
        nc.sync.dma_start(out=x_raw[3][:], in_=x_rows[3])
        nc.sync.dma_start(out=bias_rows[0:N_TILES, :], in_=b_reward.rearrange("(c p) -> c p", p=P))
        nc.sync.dma_start(out=bias_rows[N_TILES : 2 * N_TILES, :], in_=b_cont.rearrange("(c p) -> c p", p=P))
        nc.sync.dma_start(out=weights[:], in_=step_weight.partition_broadcast(P))
        for i in range(S_TILES):
            f_raw[i] = work.tile([P, T], BF16, tag="raw", bufs=6, name="f_raw")
            nc.sync.dma_start(out=f_raw[i][:], in_=filters[P * i : P * (i + 1), :])
        nc.sync.dma_start(out=boot_sb[:], in_=boot.rearrange("(i p) n -> p i n", p=P))

        make_identity(nc, ident[:])
        make_identity(nc, ident_bf[:])

        x_wide, x_turned, x_grouped = {}, {}, {}

        def widen_x(g, s, engine):
            x_wide[g, s] = work.tile([P, K], BF16, tag="x_wide", bufs=6, name="x_wide")
            source = x_raw[g][:, s, :].bitcast(FP8)
            if engine == "scalar":
                nc.scalar.copy(out=x_wide[g, s][:], in_=source)
            elif engine == "vector":
                nc.vector.tensor_copy(out=x_wide[g, s][:], in_=source)
            else:
                nc.gpsimd.tensor_copy(out=x_wide[g, s][:], in_=source)

        def pair_scales():
            for e in range(2):
                nc.vector.tensor_copy(
                    out=x_scale_pairs[:, :, 2 * e : 2 * e + 2, :],
                    in_=x_scale_raw[:].rearrange("p q (u v) -> p q u v", v=2),
                )

        def turn_x(g, h):
            for q in range(K_PASSES):
                bank = head_bank([P, 4, P]) if g < 2 else sum_bank([P, 4, P])
                for e in range(2):
                    words = x_wide[g, 2 * h + e][:].bitcast(F32)
                    for u in range(2):
                        nc.tensor.transpose(bank[:, 2 * e + u, :], words[:, 256 * q + u : 256 * (q + 1) : 2], ident[:])
                x_turned[g, h, q] = bank

        def scale_x(g, h):
            if h == 0:
                x_grouped[g] = work.tile([P, K_PASSES, BLOCK, PACK], BF16, tag="x_grouped", bufs=2, align_bytes=64, name="x_grouped")
            for q in range(K_PASSES):
                half = x_grouped[g][:, q, 256 * h : 256 * (h + 1), :].rearrange("p c t -> p (c t)")
                nc.vector.tensor_tensor(
                    out=half.rearrange("p (c w v) -> p c w v", w=4, v=2),
                    in0=x_turned[g, h, q][:].bitcast(BF16).rearrange("p w (c v) -> p c w v", v=2),
                    in1=x_scale_pairs[:, q, :, :].unsqueeze(1).to_broadcast([P, P, 4, 2]),
                    op=ALU.mult,
                )

        def quantise_x(g):
            passes = slice(K_PASSES * g, K_PASSES * (g + 1))
            nc.vector.quantize_mx(
                out=x_codes[:, passes, :].rearrange("p q c -> p (q c)").bitcast(FP8X4),
                scales=x_scales[:, passes, :].rearrange("p q c -> p (q c)"),
                in_=x_grouped[g][:].rearrange("p q c t -> p (q c t)"),
            )

        w_grouped = {}

        def group_w(i):
            q, head = i // 2, i % 2
            if head == 0:
                w_grouped[q] = work.tile([P, 2, N, PACK], BF16, tag="w_grouped", bufs=2, align_bytes=64, name="w_grouped")
            nc.scalar.copy(
                out=w_grouped[q][:, head, :, :].rearrange("p (c i) j -> p c j i", i=4),
                in_=w_raw[i][:].rearrange("p j (c i) -> p c j i", i=4),
            )

        def quantise_w(q):
            heads = slice(2 * q, 2 * q + 2)
            nc.vector.quantize_mx(
                out=w_codes[:, heads, :].rearrange("p i n -> p (i n)").bitcast(FP8X4),
                scales=w_scales[:, heads, :].rearrange("p i n -> p (i n)"),
                in_=w_grouped[q][:].rearrange("p i n j -> p (i n j)"),
            )

        def bias_columns():
            turned = turn_bank([P, P], BF16)
            nc.tensor.transpose(turned[:], bias_rows[:], ident_bf[:])
            for group, source, factor, added in ((0, 0, 1.0, 0.0), (1, 1, -0.5, 0.0), (2, 0, -1.0, -math.log(2.0))):
                nc.vector.tensor_scalar(
                    out=bias[:, N_TILES * group : N_TILES * (group + 1)],
                    in0=turned[:, N_TILES * source : N_TILES * (source + 1)],
                    scalar1=factor,
                    scalar2=added,
                    op0=ALU.mult,
                    op1=ALU.add,
                )

        f_words = f_grouped[:].rearrange("p g s t -> p (g s t)").bitcast(F32)
        f_words = f_words.rearrange("p (g s u) -> p g s u", g=T_BLOCKS, u=2)

        def turn_filters(i):
            words = f_raw[i][:].bitcast(F32)
            for h in range(2):
                bank = turn_bank([P, 4, P])
                for g in range(2):
                    first = 256 * (2 * h + g)
                    for u in range(2):
                        nc.tensor.transpose(bank[:, 2 * g + u, :], words[:, first + u : first + 256 : 2], ident[:])
                nc.scalar.copy(
                    out=f_words[:, 2 * h : 2 * h + 2, P * i : P * (i + 1), :],
                    in_=bank[:].rearrange("p (g u) s -> p g s u", u=2),
                )

        def quantise_filters(h):
            blocks = slice(2 * h, 2 * h + 2)
            nc.vector.quantize_mx(
                out=f_codes[:, blocks, :].rearrange("p g s -> p (g s)").bitcast(FP8X4),
                scales=f_scales[:, blocks, :].rearrange("p g s -> p (g s)"),
                in_=f_grouped[:, blocks, :, :].rearrange("p g s t -> p (g s t)"),
            )

        zc, zr, tanh_neg, exp_pos, exp_neg, c_minus2, cy, cy_turned, cy_grouped = {}, {}, {}, {}, {}, {}, {}, {}, {}
        cy_codes, cy_scales = {}, {}

        def multiply_heads(k):
            j, g = UNITS[k]
            cols = slice(P * j, P * (j + 1))
            for head, store in ((0, zc), (1, zr)):
                store[k] = head_bank([P, BLOCK])
                for q in range(K_PASSES):
                    nc.tensor.matmul_mx(
                        out=store[k][:],
                        lhsT=w_codes[:, 2 * q + head, cols].bitcast(FP8X4),
                        lhsT_scale=w_scales[:, 2 * q + head, cols],
                        rhs=x_codes[:, K_PASSES * g + q, :].bitcast(FP8X4),
                        rhs_scale=x_scales[:, K_PASSES * g + q, :],
                        start=(q == 0),
                        stop=(q == K_PASSES - 1),
                    )

        def activate(out, source, k, func, group, factor):
            column = N_TILES * group + UNITS[k][0]
            nc.scalar.activation(out=out[:], in_=source[:], func=func, bias=bias[:, column : column + 1], scale=factor)

        def take_tanh(k):
            tanh_neg[k] = work.tile([P, BLOCK], F32, tag="tanh_neg", bufs=3, name="tanh_neg")
            activate(tanh_neg[k], zc[k], k, ACT.Tanh, 1, -0.5)

        def take_exp_pos(k):
            exp_pos[k] = work.tile([P, BLOCK], F32, tag="exp_pos", bufs=3, name="exp_pos")
            activate(exp_pos[k], zr[k], k, ACT.Exp, 0, 1.0)

        def take_exp_neg(k):
            exp_neg[k] = work.tile([P, BLOCK], F32, tag="exp_neg", bufs=3, name="exp_neg")
            activate(exp_neg[k], zr[k], k, ACT.Exp, 2, -1.0)

        def weigh(k):
            g = UNITS[k][1]
            c_minus2[k] = work.tile([P, BLOCK], F32, tag="c_minus2", bufs=2, name="c_minus2")
            w_cols = weights[:, BLOCK * g : BLOCK * (g + 1)].rearrange("p (c h e) -> p h c e", h=2, e=2)
            for h in range(2):
                half = slice(256 * h, 256 * (h + 1))
                nc.vector.scalar_tensor_tensor(
                    out=c_minus2[k][:, half].rearrange("p (c e) -> p c e", e=2),
                    in0=tanh_neg[k][:, half].rearrange("p (c e) -> p c e", e=2),
                    scalar=1.0,
                    in1=w_cols[:, h, :, :],
                    op0=ALU.subtract,
                    op1=ALU.mult,
                )

        def round_c(k):
            cy[k] = work.tile([P, 2, BLOCK], BF16, tag="cy", bufs=3, name="cy")
            if k in ROUND_ON_SCALAR:
                nc.scalar.activation(out=cy[k][:, 0, :], in_=c_minus2[k][:], func=ACT.Copy, scale=-0.5)
            else:
                nc.vector.tensor_scalar(out=cy[k][:, 0, :], in0=c_minus2[k][:], scalar1=-0.5, scalar2=None, op0=ALU.mult)

        def multiply_c(k):
            nc.vector.scalar_tensor_tensor(
                out=exp_pos[k][:], in0=exp_pos[k][:], scalar=1.0, in1=c_minus2[k][:], op0=ALU.max, op1=ALU.mult
            )

        def make_y(k):
            nc.vector.scalar_tensor_tensor(
                out=cy[k][:, 1, :], in0=exp_neg[k][:], scalar=0.5, in1=exp_pos[k][:], op0=ALU.subtract, op1=ALU.mult
            )

        def turn_cy(k, kinds):
            cy_turned[k, kinds[0]] = turn_bank([P, len(kinds), 2, P])
            for n, kind in enumerate(kinds):
                words = cy[k][:, kind, :].bitcast(F32)
                for h in range(2):
                    nc.tensor.transpose(cy_turned[k, kinds[0]][:, n, h, :], words[:, P * h : P * (h + 1)], ident[:])

        def group_cy(k, kinds):
            if kinds[0] == 0:
                cy_grouped[k] = work.tile([P, 2, P, PACK], BF16, tag="cy_grouped", bufs=3, align_bytes=64, name="cy_grouped")
            part = cy_grouped[k][:, kinds[0] : kinds[0] + len(kinds), :, :]
            nc.scalar.copy(
                out=part.rearrange("p w n t -> p (w n t)").bitcast(F32).rearrange("p (w n h) -> p w n h", n=P, h=2),
                in_=cy_turned[k, kinds[0]][:].rearrange("p w h n -> p w n h"),
            )

        def quantise_cy(k, kinds):
            j, g = UNITS[k]
            if g == 0:
                cy_codes[j] = work.tile([P, T_BLOCKS, 2 * P], U32, tag="cy_codes", bufs=3, align_bytes=64, name="cy_codes")
                cy_scales[j] = work.tile([P, T_BLOCKS, 2 * P], U8, tag="cy_scales", bufs=3, align_bytes=64, name="cy_scales")
            cols = slice(P * kinds[0], P * (kinds[0] + len(kinds)))
            nc.vector.quantize_mx(
                out=cy_codes[j][:, g, cols].bitcast(FP8X4),
                scales=cy_scales[j][:, g, cols],
                in_=cy_grouped[k][:, kinds[0] : kinds[0] + len(kinds), :, :].rearrange("p w n t -> p (w n t)"),
            )

        mass_rows = out_1.rearrange("(i p) n -> p i n", p=P)
        ret_rows = out_0.rearrange("(i p) n -> p i n", p=P)
        sums, boot_terms, returns = {}, {}, {}

        def task_cols(j):
            return slice(P * j, P * (j + 1))

        def sum_pass(j, i, g, out):
            nc.tensor.matmul_mx(
                out=out,
                lhsT=f_codes[:, g, P * i : P * (i + 1)].bitcast(FP8X4),
                lhsT_scale=f_scales[:, g, P * i : P * (i + 1)],
                rhs=cy_codes[j][:, g, :].bitcast(FP8X4),
                rhs_scale=cy_scales[j][:, g, :],
                start=(g == 0),
                stop=(g == T_BLOCKS - 1),
            )

        def sum_half(j, h):
            sums[j, h] = sum_bank([P, 2, 2 * P])
            for i in range(2):
                for g in range(T_BLOCKS):
                    sum_pass(j, 2 * h + i, g, sums[j, h][:, i, :])

        def bootstrap(j, h):
            rows, cols = slice(2 * h, 2 * h + 2), task_cols(j)
            mass = work.tile([P, 2, P], F32, tag="mass", bufs=2, name="mass")
            nc.scalar.copy(out=mass[:], in_=sums[j, h][:, :, 0:P])
            nc.sync.dma_start(out=mass_rows[:, rows, cols], in_=mass[:])
            boot_terms[j, h] = work.tile([P, 2, P], F32, tag="boot_term", bufs=2, name="boot_term")
            nc.vector.tensor_tensor(
                out=boot_terms[j, h][:], in0=sums[j, h][:, :, 0:P], in1=boot_sb[:, rows, cols], op=ALU.mult
            )

        def add_gain(j, h):
            if h == 0:
                returns[j] = work.tile([P, S_TILES, P], F32, tag="returns", bufs=2, name="returns")
            nc.vector.tensor_tensor(
                out=returns[j][:, 2 * h : 2 * h + 2, :], in0=sums[j, h][:, :, P : 2 * P], in1=boot_terms[j, h][:], op=ALU.add
            )

        def magnitude(j):
            nc.scalar.activation(out=log_sb[:, :, task_cols(j)], in_=returns[j][:], func=ACT.Abs)

        def sign_on_scalar(j):
            nc.scalar.activation(out=sign_sb[:, :, task_cols(j)], in_=returns[j][:], func=ACT.Sign)

        def half_sign_on_vector(j):
            nc.vector.tensor_scalar(
                out=sign_sb[:, :, task_cols(j)], in0=returns[j][:], scalar1=0.0, scalar2=0.5, op0=ALU.is_ge, op1=ALU.subtract
            )

        def take_log(cols):
            nc.scalar.activation(out=log_sb[:, :, cols], in_=log_sb[:, :, cols], func=ACT.Ln, bias=1.0, scale=1.0)

        def store_returns(cols, factor):
            nc.vector.scalar_tensor_tensor(
                out=log_sb[:, :, cols],
                in0=sign_sb[:, :, cols],
                scalar=factor,
                in1=log_sb[:, :, cols],
                op0=ALU.mult,
                op1=ALU.mult,
            )
            nc.sync.dma_start(out=ret_rows[:, :, cols], in_=log_sb[:, :, cols])

        for s in range(4):
            widen_x(0, s, "vector" if s % 2 == 0 else "scalar")
            if s == 0:
                pair_scales()
            if s % 2 == 1:
                turn_x(0, s // 2)
        widen_x(1, 0, "scalar")
        for g, s in [(1, 1), (1, 2), (1, 3), (2, 0), (2, 1), (2, 2), (2, 3)]:
            widen_x(g, s, "gpsimd")
        for h in range(2):
            scale_x(0, h)
            group_w(h)
        for h in range(2):
            turn_x(1, h)
            scale_x(1, h)
        quantise_x(0)
        group_w(2)
        bias_columns()
        group_w(3)
        turn_x(2, 0)
        widen_x(3, 0, "scalar")
        scale_x(2, 0)
        turn_filters(0)
        quantise_w(0)
        quantise_w(1)
        turn_x(2, 1)
        widen_x(3, 1, "scalar")
        scale_x(2, 1)
        quantise_x(1)
        multiply_heads(0)
        widen_x(3, 2, "scalar")
        take_tanh(0)
        take_exp_pos(0)
        take_exp_neg(0)
        widen_x(3, 3, "scalar")
        turn_filters(1)
        turn_x(3, 0)
        multiply_heads(1)
        weigh(0)

        both = range(2)
        for k in range(LAST):
            if k >= 1:
                turn_cy(k - 1, both)
            if k + 2 <= LAST:
                multiply_heads(k + 2)
            take_tanh(k + 1)
            take_exp_pos(k + 1)
            multiply_c(k)
            round_c(k)
            if k in FINISH_AT:
                bootstrap(*FINISH_AT[k])
            if k >= 1:
                group_cy(k - 1, both)
            take_exp_neg(k + 1)
            if k <= 1:
                scale_x(3, k)
            if k in FILTERS_QUANTISED_AT:
                quantise_filters(FILTERS_QUANTISED_AT[k])
            make_y(k)
            weigh(k + 1)
            if k >= 1:
                quantise_cy(k - 1, both)
            if k == 0:
                turn_x(3, 1)
            if k in FILTERS_TURNED_AT:
                turn_filters(FILTERS_TURNED_AT[k])
            if k == 0:
                quantise_x(2)
            if k == 2:
                quantise_x(3)
            if k in FINISH_AT:
                add_gain(*FINISH_AT[k])
            if k in SUMS_AT:
                sum_half(*SUMS_AT[k])
            if k in MAGNITUDE_AT:
                magnitude(MAGNITUDE_AT[k])
                sign_on_scalar(MAGNITUDE_AT[k])

        early, late = slice(0, 2 * P), slice(2 * P, 3 * P)
        tail_cols = task_cols(3)
        tail = [head_bank([P, 2 * P]) for i in range(S_TILES)]

        def tail_passes(g):
            for i in range(S_TILES):
                sum_pass(3, i, g, tail[i][:])

        turn_cy(LAST - 1, both)
        group_cy(LAST - 1, both)
        take_log(early)
        round_c(LAST)
        multiply_c(LAST)
        tail_passes(0)
        tail_passes(1)
        turn_cy(LAST, range(0, 1))
        group_cy(LAST, range(0, 1))
        bootstrap(2, 1)
        quantise_cy(LAST - 1, both)
        add_gain(2, 1)
        tail_passes(2)
        make_y(LAST)
        turn_cy(LAST, range(1, 2))
        group_cy(LAST, range(1, 2))
        half_sign_on_vector(2)
        quantise_cy(LAST, range(0, 1))
        quantise_cy(LAST, range(1, 2))
        magnitude(2)
        take_log(late)
        tail_passes(3)

        tail_mass = work.tile([P, S_TILES, P], F32, tag="mass", bufs=2, name="tail_mass")
        tail_boot = work.tile([P, S_TILES, P], F32, tag="boot_term", bufs=2, name="tail_boot")
        returns[3] = work.tile([P, S_TILES, P], F32, tag="returns", bufs=2, name="returns")
        store_returns(early, 1.0)
        for i in range(S_TILES + 1):
            if i < S_TILES:
                nc.vector.tensor_tensor(
                    out=tail_boot[:, i, :], in0=tail[i][:, 0:P], in1=boot_sb[:, i, tail_cols], op=ALU.mult
                )
            if i >= 1:
                nc.vector.tensor_tensor(
                    out=returns[3][:, i - 1, :], in0=tail[i - 1][:, P : 2 * P], in1=tail_boot[:, i - 1, :], op=ALU.add
                )
        for i in range(S_TILES):
            nc.scalar.copy(out=tail_mass[:, i, :], in_=tail[i][:, 0:P])
        nc.sync.dma_start(out=mass_rows[:, :, tail_cols], in_=tail_mass[:])
        magnitude(3)
        take_log(tail_cols)
        store_returns(late, 2.0)
        half_sign_on_vector(3)
        store_returns(tail_cols, 2.0)
